import numpy as np
import ml_dtypes


def mxq(x, axis, fmt="e4m3"):
    dtype, down = {"e4m3": (ml_dtypes.float8_e4m3fn, 7), "e5m2": (ml_dtypes.float8_e5m2, 14)}[fmt]
    v = np.moveaxis(np.asarray(x, np.float32).astype(ml_dtypes.bfloat16).astype(np.float64), axis, -1)
    blocks = v.reshape(v.shape[:-1] + (-1, 32))
    amax = np.abs(blocks).max(-1, keepdims=True)
    byte = np.maximum(np.where(amax > 0, np.frexp(amax)[1] - 1 + 127, 0) - down, 1)
    scale = np.exp2(byte - 127.0)
    codes = (blocks / scale).astype(np.float32).astype(dtype).astype(np.float64)
    return np.moveaxis((codes * scale).reshape(v.shape), -1, axis)


WIDE = False


def mx_kscale(k):
    if not WIDE:
        return np.ones(k)
    levels = np.array([10, -10, 5, -5, 0])
    if k % 512:
        return np.exp2(np.random.permutation(np.resize(levels, k // 32))).repeat(32)
    a = np.empty((k // 512, 16))
    for p in range(k // 512):
        a[p, :8] = np.random.permutation(np.resize(levels, 8))
        for g in range(8):
            far = levels[np.abs(levels - a[p, g]) >= 10]
            a[p, g + 8] = far[np.random.randint(len(far))]
    return np.exp2(a.ravel()).repeat(32)


def f64(x):
    return np.asarray(x).astype(np.float64)


def striped(idx):
    return np.tile(idx.reshape(-1, 16).T, (8, 1)).astype(np.uint16)


def unstriped(offs):
    return offs[:16].T.reshape(-1).astype(np.int64)


def pack_weight(w):
    k, n = w.shape
    w = f64(np.asarray(w, np.float32).astype(ml_dtypes.bfloat16)).reshape(k // 32, 32, n)
    amax = np.abs(w).max(1)
    byte = np.clip(np.where(amax > 0, np.frexp(amax)[1] - 1 + 127 - 7, 1), 1, 254)
    scaled = (w * np.exp2(127.0 - byte)[:, None, :]).reshape(k, n).astype(np.float32)
    words = np.ascontiguousarray(scaled.reshape(k // 512, 128, 4, n).transpose(0, 1, 3, 2)).astype(ml_dtypes.float8_e4m3fn).view(np.uint8)
    return words, np.ascontiguousarray(byte.astype(np.uint8).reshape(k // 512, 16, n))


def unpack_weight(words, scales):
    g, p, n, _ = words.shape
    vals = np.ascontiguousarray(words).view(ml_dtypes.float8_e4m3fn).astype(np.float64) * np.repeat(np.exp2(scales.astype(np.float64) - 127.0), 8, axis=1)[..., None]
    return vals.transpose(0, 1, 3, 2).reshape(g * 512, n)


def relu(v):
    return np.maximum(v, 0.0)


K, T, S, N, D = 512, 4096, 1024, 512, 4


def setup_inputs():
    n = np.random.standard_normal
    s = mx_kscale(K)[:, None]
    packed_xT = pack_weight(n((K, T)) * s)
    return {
        "x_words": packed_xT[0],
        "x_scales": packed_xT[1],
        "w1": (n((K, N)) / np.sqrt(K) / s).astype(np.float32),
        "bias": (0.3 * n((N, 1))).astype(np.float32),
        "offs": striped(np.random.permutation(T)[:S]),
    }


def reference(x_words, x_scales, w1, bias, offs):
    xq = unpack_weight(x_words, x_scales)[:, unstriped(offs)]
    y = np.log(relu((mxq(f64(w1), 0, "e4m3").T @ xq) + f64(bias)) + 1.0)
    return y.reshape(len(y), -1, D).max(axis=2)

@@ -1,0 +1,113 @@
+from contextlib import ExitStack
+
+import concourse.mybir as mybir
+
+K, T, S, N, D = 512, 4096, 1024, 512, 4
+FLOPS = 2 * K * N * S
+
+F32 = mybir.dt.float32
+BF16 = mybir.dt.bfloat16
+I32 = mybir.dt.int32
+U32 = mybir.dt.uint32
+U16 = mybir.dt.uint16
+U8 = mybir.dt.uint8
+FP8X4 = mybir.dt.float8_e4m3fn_x4
+ACT = mybir.ActivationFunctionType
+ALU = mybir.AluOpType
+
+P = 128
+PACK = 4
+HALF = 512
+DOCS = HALF // D
+TILES = N // P
+FIRST = 1024
+
+
+def tile_picked_ysplade_max_p_kernel(tc, x_words, x_scales, w1, bias, offs, out):
+    nc = tc.nc
+    with ExitStack() as ctx:
+        keep = ctx.enter_context(tc.tile_pool(name="keep", bufs=1))
+        psum = ctx.enter_context(tc.psum_pool(name="psum", bufs=1))
+
+        offsets = keep.tile([P, S // 16], U16, name="offsets")
+        nc.sync.dma_start(offsets[:], offs)
+
+        table = keep.tile([P, T], I32, name="table", tag="words", align_bytes=64)
+        words = x_words[0].rearrange("p n t -> p (n t)").bitcast(I32)
+        nc.sync.dma_start(table[:, :FIRST], words[:, :FIRST])
+
+        scale_table = keep.tile([P, T], U8, name="scale_table", tag="scales", align_bytes=64)
+        nc.vector.memset(scale_table[:].bitcast(I32), 0)
+        s_rows = x_scales[0].bitcast(I32).rearrange("(q r) c -> r q c", r=4)
+        for r in range(4):
+            nc.sync.dma_start(scale_table[r:P:32, :].bitcast(I32), s_rows[r])
+        nc.sync.dma_start(table[:, FIRST:], words[:, FIRST:])
+
+        w_rows = w1.rearrange("(p j) n -> p j n", j=PACK)
+        w_raw = []
+        for h in range(2):
+            raw = keep.tile([P, PACK, 2 * P], F32, name="w_raw%d" % h)
+            nc.sync.dma_start(raw[:], w_rows[:, :, 2 * P * h : 2 * P * (h + 1)])
+            w_raw.append(raw)
+
+        b_col = keep.tile([P, TILES], F32, name="b_col")
+        with nc.allow_non_contiguous_dma(reason="one bias a partition"):
+            nc.scalar.dma_start(b_col[:], bias.rearrange("(t p) o -> p (t o)", p=P))
+
+        x_sc = keep.tile([P, S], U8, name="x_sc", align_bytes=64)
+        nc.vector.tensor_copy(x_sc[:], scale_table[:].indirect(offsets[:]))
+
+        x_codes = keep.tile([P, S], U32, name="x_codes", tag="scales", align_bytes=64)
+        for h in range(2):
+            nc.vector.tensor_copy(x_codes[:, HALF * h : HALF * (h + 1)], table[:].bitcast(U32).indirect(offsets[:, 32 * h : 32 * (h + 1)]))
+
+        w_codes = keep.tile([P, N], U32, name="w_codes", tag="words", align_bytes=64)
+        w_sc = keep.tile([P, N], U8, name="w_sc", align_bytes=64)
+
+        def quantise(t):
+            grouped = keep.tile([P, P, PACK], BF16, name="grouped%d" % t, align_bytes=64)
+            src = w_raw[t // 2][:, :, P * (t % 2) : P * (t % 2 + 1)].rearrange("p j m -> p m j")
+            if t < 2:
+                nc.scalar.copy(grouped[:], src)
+            else:
+                nc.gpsimd.tensor_scalar(grouped[:], src, 1.0, 0.0, ALU.mult, ALU.add)
+            cols = slice(P * t, P * (t + 1))
+            nc.vector.quantize_mx(out=w_codes[:, cols].bitcast(FP8X4), scales=w_sc[:, cols], in_=grouped[:].rearrange("p m j -> p (m j)"))
+
+        def product(t, h):
+            cols = slice(P * t, P * (t + 1))
+            entries = slice(HALF * h, HALF * (h + 1))
+            acc = psum.tile([P, HALF], F32, name="acc%d_%d" % (t, h))
+            nc.tensor.matmul_mx(
+                out=acc[:],
+                lhsT=w_codes[:, cols].bitcast(FP8X4),
+                lhsT_scale=w_sc[:, cols],
+                rhs=x_codes[:, entries].bitcast(FP8X4),
+                rhs_scale=x_sc[:, entries],
+                start=True,
+                stop=True,
+            )
+            return acc[:].rearrange("p (v d) -> p d v", d=D)
+
+        quantise(0)
+        quantise(1)
+        banks, best = [], []
+        for step in range(2 * TILES + 2):
+            if step < 2 * TILES:
+                t, h = divmod(step, 2)
+                if h == 0:
+                    best.append(keep.tile([P, D, 2 * DOCS], F32, name="best%d" % t))
+                banks.append(product(t, h))
+                nc.scalar.activation(best[t][:, 0, DOCS * h : DOCS * (h + 1)], banks[step][:, 0, :], ACT.Relu, bias=b_col[:, t : t + 1])
+            for d in range(1, D):
+                i = step - d + 1
+                if 0 <= i < 2 * TILES:
+                    t, h = divmod(i, 2)
+                    docs = slice(DOCS * h, DOCS * (h + 1))
+                    nc.vector.scalar_tensor_tensor(best[t][:, d, docs], banks[i][:, d, :], b_col[:, t : t + 1], best[t][:, d - 1, docs], ALU.add, ALU.max)
+                    if d == D - 1 and h == 1:
+                        y = keep.tile([P, 2 * DOCS], F32, name="y%d" % t)
+                        nc.scalar.activation(y[:], best[t][:, D - 1, :], ACT.Ln, bias=1.0)
+                        nc.sync.dma_start(out[P * t : P * (t + 1), :], y[:])
+            if step in (0, 2):
+                quantise(2 + step // 2)

@@ -20,7 +20,6 @@ PACK = 4
 HALF = 512
 DOCS = HALF // D
 TILES = N // P
-FIRST = 1024
 
 
 def tile_picked_ysplade_max_p_kernel(tc, x_words, x_scales, w1, bias, offs, out):
@@ -32,56 +31,61 @@ def tile_picked_ysplade_max_p_kernel(tc, x_words, x_scales, w1, bias, offs, out)
         offsets = keep.tile([P, S // 16], U16, name="offsets")
         nc.sync.dma_start(offsets[:], offs)
 
-        table = keep.tile([P, T], I32, name="table", tag="words", align_bytes=64)
-        words = x_words[0].rearrange("p n t -> p (n t)").bitcast(I32)
-        nc.sync.dma_start(table[:, :FIRST], words[:, :FIRST])
+        w_rows = w1.rearrange("(p j) n -> p j n", j=PACK)
+        w_early = keep.tile([P, PACK, 2 * P], F32, name="w_early")
+        nc.sync.dma_start(w_early[:], w_rows[:, :, : 2 * P])
+        w_late = [keep.tile([P, PACK, P], F32, name="w_late%d" % h, tag="late%d" % h) for h in range(2)]
+        w_raw = [w_early[:, :, :P], w_early[:, :, P:], w_late[0][:], w_late[1][:]]
 
         scale_table = keep.tile([P, T], U8, name="scale_table", tag="scales", align_bytes=64)
         nc.vector.memset(scale_table[:].bitcast(I32), 0)
-        s_rows = x_scales[0].bitcast(I32).rearrange("(q r) c -> r q c", r=4)
-        for r in range(4):
-            nc.sync.dma_start(scale_table[r:P:32, :].bitcast(I32), s_rows[r])
-        nc.sync.dma_start(table[:, FIRST:], words[:, FIRST:])
+        nc.sync.dma_start(scale_table[0:P:8, :].bitcast(I32), x_scales[0].bitcast(I32))
 
-        w_rows = w1.rearrange("(p j) n -> p j n", j=PACK)
-        w_raw = []
-        for h in range(2):
-            raw = keep.tile([P, PACK, 2 * P], F32, name="w_raw%d" % h)
-            nc.sync.dma_start(raw[:], w_rows[:, :, 2 * P * h : 2 * P * (h + 1)])
-            w_raw.append(raw)
+        table = keep.tile([P, T], I32, name="table")
+        nc.sync.dma_start(table[:], x_words[0].rearrange("p n t -> p (n t)").bitcast(I32))
 
+        nc.sync.dma_start(w_late[0][:], w_rows[:, :, 2 * P : 3 * P])
         b_col = keep.tile([P, TILES], F32, name="b_col")
         with nc.allow_non_contiguous_dma(reason="one bias a partition"):
-            nc.scalar.dma_start(b_col[:], bias.rearrange("(t p) o -> p (t o)", p=P))
+            nc.sync.dma_start(b_col[:], bias.rearrange("(t p) o -> p (t o)", p=P))
+        nc.sync.dma_start(w_late[1][:], w_rows[:, :, 3 * P :])
 
+        one = keep.tile([P, 1], F32, name="one")
+        nc.gpsimd.memset(one[:], 1.0)
+        warm = keep.tile([P, 1], F32, name="warm")
+        nc.scalar.activation(warm[:], one[:], ACT.Ln)
+
+        picked_sc = keep.tile([P, S], U8, name="picked_sc", align_bytes=64)
+        nc.vector.tensor_copy(picked_sc[:], scale_table[:].indirect(offsets[:]))
         x_sc = keep.tile([P, S], U8, name="x_sc", align_bytes=64)
-        nc.vector.tensor_copy(x_sc[:], scale_table[:].indirect(offsets[:]))
+        nc.vector.tensor_copy(x_sc[:].bitcast(I32), picked_sc[:].bitcast(I32))
+        for r in range(1, 4):
+            nc.scalar.dma_start(x_sc[r:P:32, :].bitcast(I32), picked_sc[8 * r : P : 32, :].bitcast(I32))
+
+        w_codes, w_sc = [], []
+
+        def quantise(t):
+            grouped = keep.tile([P, P, PACK], BF16, name="grouped%d" % t, align_bytes=64)
+            src = w_raw[t]
+            nc.scalar.copy(grouped[:].rearrange("p (c i) j -> p c j i", i=4), src.rearrange("p j (c i) -> p c j i", i=4))
+            w_codes.append(keep.tile([P, P], U32, name="w_codes%d" % t, align_bytes=64))
+            w_sc.append(keep.tile([P, P], U8, name="w_sc%d" % t, align_bytes=64))
+            nc.vector.quantize_mx(out=w_codes[t][:].bitcast(FP8X4), scales=w_sc[t][:], in_=grouped[:].rearrange("p m j -> p (m j)"))
+
+        quantise(0)
+        quantise(1)
 
         x_codes = keep.tile([P, S], U32, name="x_codes", tag="scales", align_bytes=64)
         for h in range(2):
             nc.vector.tensor_copy(x_codes[:, HALF * h : HALF * (h + 1)], table[:].bitcast(U32).indirect(offsets[:, 32 * h : 32 * (h + 1)]))
 
-        w_codes = keep.tile([P, N], U32, name="w_codes", tag="words", align_bytes=64)
-        w_sc = keep.tile([P, N], U8, name="w_sc", align_bytes=64)
-
-        def quantise(t):
-            grouped = keep.tile([P, P, PACK], BF16, name="grouped%d" % t, align_bytes=64)
-            src = w_raw[t // 2][:, :, P * (t % 2) : P * (t % 2 + 1)].rearrange("p j m -> p m j")
-            if t < 2:
-                nc.scalar.copy(grouped[:], src)
-            else:
-                nc.gpsimd.tensor_scalar(grouped[:], src, 1.0, 0.0, ALU.mult, ALU.add)
-            cols = slice(P * t, P * (t + 1))
-            nc.vector.quantize_mx(out=w_codes[:, cols].bitcast(FP8X4), scales=w_sc[:, cols], in_=grouped[:].rearrange("p m j -> p (m j)"))
-
         def product(t, h):
-            cols = slice(P * t, P * (t + 1))
             entries = slice(HALF * h, HALF * (h + 1))
             acc = psum.tile([P, HALF], F32, name="acc%d_%d" % (t, h))
             nc.tensor.matmul_mx(
                 out=acc[:],
-                lhsT=w_codes[:, cols].bitcast(FP8X4),
-                lhsT_scale=w_sc[:, cols],
+                lhsT=w_codes[t][:].bitcast(FP8X4),
+                lhsT_scale=w_sc[t][:],
                 rhs=x_codes[:, entries].bitcast(FP8X4),
                 rhs_scale=x_sc[:, entries],
                 start=True,
@@ -89,25 +93,37 @@ def tile_picked_ysplade_max_p_kernel(tc, x_words, x_scales, w1, bias, offs, out)
             )
             return acc[:].rearrange("p (v d) -> p d v", d=D)
 
-        quantise(0)
-        quantise(1)
-        banks, best = [], []
-        for step in range(2 * TILES + 2):
-            if step < 2 * TILES:
-                t, h = divmod(step, 2)
-                if h == 0:
-                    best.append(keep.tile([P, D, 2 * DOCS], F32, name="best%d" % t))
-                banks.append(product(t, h))
-                nc.scalar.activation(best[t][:, 0, DOCS * h : DOCS * (h + 1)], banks[step][:, 0, :], ACT.Relu, bias=b_col[:, t : t + 1])
-            for d in range(1, D):
-                i = step - d + 1
-                if 0 <= i < 2 * TILES:
-                    t, h = divmod(i, 2)
-                    docs = slice(DOCS * h, DOCS * (h + 1))
-                    nc.vector.scalar_tensor_tensor(best[t][:, d, docs], banks[i][:, d, :], b_col[:, t : t + 1], best[t][:, d - 1, docs], ALU.add, ALU.max)
-                    if d == D - 1 and h == 1:
-                        y = keep.tile([P, 2 * DOCS], F32, name="y%d" % t)
-                        nc.scalar.activation(y[:], best[t][:, D - 1, :], ACT.Ln, bias=1.0)
-                        nc.sync.dma_start(out[P * t : P * (t + 1), :], y[:])
+        order = [(0, 0), (1, 0), (0, 1), (1, 1), (2, 0), (2, 1), (3, 0), (3, 1)]
+        ys = [keep.tile([P, 2 * DOCS], F32, name="y%d" % t) for t in range(TILES)]
+
+        def finish(t, h, best):
+            if t == TILES - 1:
+                docs = slice(DOCS * h, DOCS * (h + 1))
+                nc.scalar.activation(ys[t][:, docs], best[:, docs], ACT.Ln, bias=1.0)
+                nc.sync.dma_start(out[P * t : P * (t + 1), docs], ys[t][:, docs])
+            elif h == 1:
+                nc.scalar.activation(ys[t][:], best, ACT.Ln, bias=1.0)
+                nc.sync.dma_start(out[P * t : P * (t + 1), :], ys[t][:])
+
+        best = [keep.tile([P, D - 1, 2 * DOCS], F32, name="best%d" % t) for t in range(TILES)]
+        banks, first = [], []
+        for step in range(len(order) + 2):
             if step in (0, 2):
                 quantise(2 + step // 2)
+                held = keep.tile([P, 2, DOCS], F32, name="first%d" % step, tag="late%d" % (step // 2))
+            elif step in (4, 6):
+                held = keep.tile([P, 2, DOCS], F32, name="first%d" % step)
+            if step < len(order):
+                t, h = order[step]
+                banks.append(product(t, h))
+                first.append(held[:, step % 2, :])
+                nc.scalar.activation(first[step], banks[step][:, 0, :], ACT.Relu, bias=b_col[:, t : t + 1])
+            for d in range(1, D):
+                i = step - d + 1
+                if 0 <= i < len(order):
+                    t, h = order[i]
+                    docs = slice(DOCS * h, DOCS * (h + 1))
+                    before = first[i] if d == 1 else best[t][:, d - 2, docs]
+                    nc.vector.scalar_tensor_tensor(best[t][:, d - 1, docs], banks[i][:, d, :], b_col[:, t : t + 1], before, ALU.add, ALU.max)
+                    if d == D - 1:
+                        finish(t, h, best[t][:, D - 2, :])

@@ -20,6 +20,11 @@ PACK = 4
 HALF = 512
 DOCS = HALF // D
 TILES = N // P
+LIST_GROUP = 16
+QUADRANT = 32
+BLOCK_ROWS = 8
+ROWS_AHEAD = 3
+ORDER = [(0, 0), (1, 0), (0, 1), (1, 1), (2, 0), (2, 1), (3, 0), (3, 1)]
 
 
 def tile_picked_ysplade_max_p_kernel(tc, x_words, x_scales, w1, bias, offs, out):
@@ -28,27 +33,28 @@ def tile_picked_ysplade_max_p_kernel(tc, x_words, x_scales, w1, bias, offs, out)
         keep = ctx.enter_context(tc.tile_pool(name="keep", bufs=1))
         psum = ctx.enter_context(tc.psum_pool(name="psum", bufs=1))
 
-        offsets = keep.tile([P, S // 16], U16, name="offsets")
+        offsets = keep.tile([P, S // LIST_GROUP], U16, name="offsets")
         nc.sync.dma_start(offsets[:], offs)
 
         w_rows = w1.rearrange("(p j) n -> p j n", j=PACK)
         w_early = keep.tile([P, PACK, 2 * P], F32, name="w_early")
-        nc.sync.dma_start(w_early[:], w_rows[:, :, : 2 * P])
-        w_late = [keep.tile([P, PACK, P], F32, name="w_late%d" % h, tag="late%d" % h) for h in range(2)]
+        nc.sync.dma_start(w_early[:, :ROWS_AHEAD, :], w_rows[:, :ROWS_AHEAD, : 2 * P])
+        w_late = [keep.tile([P, PACK, P], F32, name="w_late%d" % i) for i in range(2)]
         w_raw = [w_early[:, :, :P], w_early[:, :, P:], w_late[0][:], w_late[1][:]]
 
-        scale_table = keep.tile([P, T], U8, name="scale_table", tag="scales", align_bytes=64)
+        scale_table = keep.tile([P, T], U8, name="scale_table")
         nc.vector.memset(scale_table[:].bitcast(I32), 0)
-        nc.sync.dma_start(scale_table[0:P:8, :].bitcast(I32), x_scales[0].bitcast(I32))
+        nc.sync.dma_start(scale_table[0:P:BLOCK_ROWS, :].bitcast(I32), x_scales[0].bitcast(I32))
+        nc.sync.dma_start(w_early[:, ROWS_AHEAD:, :], w_rows[:, ROWS_AHEAD:, : 2 * P])
 
-        table = keep.tile([P, T], I32, name="table")
-        nc.sync.dma_start(table[:], x_words[0].rearrange("p n t -> p (n t)").bitcast(I32))
+        word_table = keep.tile([P, T], I32, name="word_table")
+        nc.sync.dma_start(word_table[:], x_words[0].rearrange("p n t -> p (n t)").bitcast(I32))
 
         nc.sync.dma_start(w_late[0][:], w_rows[:, :, 2 * P : 3 * P])
-        b_col = keep.tile([P, TILES], F32, name="b_col")
-        with nc.allow_non_contiguous_dma(reason="one bias a partition"):
-            nc.sync.dma_start(b_col[:], bias.rearrange("(t p) o -> p (t o)", p=P))
         nc.sync.dma_start(w_late[1][:], w_rows[:, :, 3 * P :])
+        b_col = keep.tile([P, TILES], F32, name="b_col")
+        with nc.allow_non_contiguous_dma(reason="one bias value a partition and term tile"):
+            nc.sync.dma_start(b_col[:], bias.rearrange("(t p) o -> p (t o)", p=P))
 
         one = keep.tile([P, 1], F32, name="one")
         nc.gpsimd.memset(one[:], 1.0)
@@ -59,15 +65,14 @@ def tile_picked_ysplade_max_p_kernel(tc, x_words, x_scales, w1, bias, offs, out)
         nc.vector.tensor_copy(picked_sc[:], scale_table[:].indirect(offsets[:]))
         x_sc = keep.tile([P, S], U8, name="x_sc", align_bytes=64)
         nc.vector.tensor_copy(x_sc[:].bitcast(I32), picked_sc[:].bitcast(I32))
-        for r in range(1, 4):
-            nc.scalar.dma_start(x_sc[r:P:32, :].bitcast(I32), picked_sc[8 * r : P : 32, :].bitcast(I32))
+        for r in range(1, QUADRANT // BLOCK_ROWS):
+            nc.scalar.dma_start(x_sc[r:P:QUADRANT, :].bitcast(I32), picked_sc[BLOCK_ROWS * r : P : QUADRANT, :].bitcast(I32))
 
         w_codes, w_sc = [], []
 
         def quantise(t):
             grouped = keep.tile([P, P, PACK], BF16, name="grouped%d" % t, align_bytes=64)
-            src = w_raw[t]
-            nc.scalar.copy(grouped[:].rearrange("p (c i) j -> p c j i", i=4), src.rearrange("p j (c i) -> p c j i", i=4))
+            nc.scalar.copy(grouped[:].rearrange("p (c i) j -> p c j i", i=4), w_raw[t].rearrange("p j (c i) -> p c j i", i=4))
             w_codes.append(keep.tile([P, P], U32, name="w_codes%d" % t, align_bytes=64))
             w_sc.append(keep.tile([P, P], U8, name="w_sc%d" % t, align_bytes=64))
             nc.vector.quantize_mx(out=w_codes[t][:].bitcast(FP8X4), scales=w_sc[t][:], in_=grouped[:].rearrange("p m j -> p (m j)"))
@@ -75,55 +80,46 @@ def tile_picked_ysplade_max_p_kernel(tc, x_words, x_scales, w1, bias, offs, out)
         quantise(0)
         quantise(1)
 
-        x_codes = keep.tile([P, S], U32, name="x_codes", tag="scales", align_bytes=64)
+        x_codes = [keep.tile([P, HALF], U32, name="x_codes%d" % h, align_bytes=64) for h in range(2)]
         for h in range(2):
-            nc.vector.tensor_copy(x_codes[:, HALF * h : HALF * (h + 1)], table[:].bitcast(U32).indirect(offsets[:, 32 * h : 32 * (h + 1)]))
+            columns = slice(h * HALF // LIST_GROUP, (h + 1) * HALF // LIST_GROUP)
+            nc.vector.tensor_copy(x_codes[h][:], word_table[:].bitcast(U32).indirect(offsets[:, columns]))
+
+        quantise(2)
+        quantise(3)
+
+        best = [keep.tile([P, 2 * DOCS], F32, name="best%d" % t) for t in range(TILES)]
+        pair = [keep.tile([P, 2, 2 * DOCS], F32, name="pair%d" % t) for t in range(TILES)]
+        y = [keep.tile([P, 2 * DOCS], F32, name="y%d" % t) for t in range(TILES)]
 
         def product(t, h):
-            entries = slice(HALF * h, HALF * (h + 1))
             acc = psum.tile([P, HALF], F32, name="acc%d_%d" % (t, h))
             nc.tensor.matmul_mx(
                 out=acc[:],
                 lhsT=w_codes[t][:].bitcast(FP8X4),
                 lhsT_scale=w_sc[t][:],
-                rhs=x_codes[:, entries].bitcast(FP8X4),
-                rhs_scale=x_sc[:, entries],
+                rhs=x_codes[h][:].bitcast(FP8X4),
+                rhs_scale=x_sc[:, HALF * h : HALF * (h + 1)],
                 start=True,
                 stop=True,
             )
-            return acc[:].rearrange("p (v d) -> p d v", d=D)
+            tokens = acc[:].rearrange("p (v d) -> p d v", d=D)
+            b = b_col[:, t : t + 1]
+            low = keep.tile([P, 2, DOCS], F32, name="low%d_%d" % (t, h))
+            nc.scalar.activation(low[:], tokens[:, 0:2, :], ACT.Relu, bias=b)
+            nc.vector.scalar_tensor_tensor(pair[t][:, :, DOCS * h : DOCS * (h + 1)], tokens[:, 2:4, :], b, low[:], ALU.add, ALU.max)
 
-        order = [(0, 0), (1, 0), (0, 1), (1, 1), (2, 0), (2, 1), (3, 0), (3, 1)]
-        ys = [keep.tile([P, 2 * DOCS], F32, name="y%d" % t) for t in range(TILES)]
+        def finish(t, docs):
+            nc.vector.tensor_tensor(best[t][:, docs], pair[t][:, 0, docs], pair[t][:, 1, docs], ALU.max)
+            nc.scalar.activation(y[t][:, docs], best[t][:, docs], ACT.Ln, bias=1.0)
+            nc.sync.dma_start(out[P * t : P * (t + 1), docs], y[t][:, docs])
 
-        def finish(t, h, best):
-            if t == TILES - 1:
-                docs = slice(DOCS * h, DOCS * (h + 1))
-                nc.scalar.activation(ys[t][:, docs], best[:, docs], ACT.Ln, bias=1.0)
-                nc.sync.dma_start(out[P * t : P * (t + 1), docs], ys[t][:, docs])
-            elif h == 1:
-                nc.scalar.activation(ys[t][:], best, ACT.Ln, bias=1.0)
-                nc.sync.dma_start(out[P * t : P * (t + 1), :], ys[t][:])
-
-        best = [keep.tile([P, D - 1, 2 * DOCS], F32, name="best%d" % t) for t in range(TILES)]
-        banks, first = [], []
-        for step in range(len(order) + 2):
-            if step in (0, 2):
-                quantise(2 + step // 2)
-                held = keep.tile([P, 2, DOCS], F32, name="first%d" % step, tag="late%d" % (step // 2))
-            elif step in (4, 6):
-                held = keep.tile([P, 2, DOCS], F32, name="first%d" % step)
-            if step < len(order):
-                t, h = order[step]
-                banks.append(product(t, h))
-                first.append(held[:, step % 2, :])
-                nc.scalar.activation(first[step], banks[step][:, 0, :], ACT.Relu, bias=b_col[:, t : t + 1])
-            for d in range(1, D):
-                i = step - d + 1
-                if 0 <= i < len(order):
-                    t, h = order[i]
-                    docs = slice(DOCS * h, DOCS * (h + 1))
-                    before = first[i] if d == 1 else best[t][:, d - 2, docs]
-                    nc.vector.scalar_tensor_tensor(best[t][:, d - 1, docs], banks[i][:, d, :], b_col[:, t : t + 1], before, ALU.add, ALU.max)
-                    if d == D - 1:
-                        finish(t, h, best[t][:, D - 2, :])
+        for step in range(len(ORDER) + 1):
+            if step < len(ORDER):
+                product(*ORDER[step])
+            if step > 0:
+                t, h = ORDER[step - 1]
+                if t == TILES - 1:
+                    finish(t, slice(DOCS * h, DOCS * (h + 1)))
+                elif h == 1:
+                    finish(t, slice(0, 2 * DOCS))

@@ -1,6 +1,7 @@
 from contextlib import ExitStack
 
 import concourse.mybir as mybir
+from concourse.masks import make_identity
 
 K, T, S, N, D = 512, 4096, 1024, 512, 4
 FLOPS = 2 * K * N * S
@@ -39,7 +40,7 @@ def tile_picked_ysplade_max_p_kernel(tc, x_words, x_scales, w1, bias, offs, out)
         w_rows = w1.rearrange("(p j) n -> p j n", j=PACK)
         w_early = keep.tile([P, PACK, 2 * P], F32, name="w_early")
         nc.sync.dma_start(w_early[:, :ROWS_AHEAD, :], w_rows[:, :ROWS_AHEAD, : 2 * P])
-        w_late = [keep.tile([P, PACK, P], F32, name="w_late%d" % i) for i in range(2)]
+        w_late = [keep.tile([P, PACK, P], F32, name="w_late%d" % i, tag="late%d" % i) for i in range(2)]
         w_raw = [w_early[:, :, :P], w_early[:, :, P:], w_late[0][:], w_late[1][:]]
 
         scale_table = keep.tile([P, T], U8, name="scale_table")
@@ -52,9 +53,16 @@ def tile_picked_ysplade_max_p_kernel(tc, x_words, x_scales, w1, bias, offs, out)
 
         nc.sync.dma_start(w_late[0][:], w_rows[:, :, 2 * P : 3 * P])
         nc.sync.dma_start(w_late[1][:], w_rows[:, :, 3 * P :])
+
+        b_rows = keep.tile([P, P], F32, name="b_rows")
+        nc.gpsimd.memset(b_rows[:], 0.0)
+        nc.scalar.dma_start(b_rows[:TILES, :], bias.rearrange("(t p) o -> t (p o)", p=P))
+        identity = keep.tile([P, P], F32, name="identity")
+        make_identity(nc, identity[:])
+        b_turned = psum.tile([P, P], F32, name="b_turned", tag="acc%d_%d" % ORDER[-1])
+        nc.tensor.transpose(b_turned[:], b_rows[:], identity[:])
         b_col = keep.tile([P, TILES], F32, name="b_col")
-        with nc.allow_non_contiguous_dma(reason="one bias value a partition and term tile"):
-            nc.sync.dma_start(b_col[:], bias.rearrange("(t p) o -> p (t o)", p=P))
+        nc.scalar.copy(b_col[:], b_turned[:, :TILES])
 
         one = keep.tile([P, 1], F32, name="one")
         nc.gpsimd.memset(one[:], 1.0)
@@ -90,10 +98,13 @@ def tile_picked_ysplade_max_p_kernel(tc, x_words, x_scales, w1, bias, offs, out)
 
         best = [keep.tile([P, 2 * DOCS], F32, name="best%d" % t) for t in range(TILES)]
         pair = [keep.tile([P, 2, 2 * DOCS], F32, name="pair%d" % t) for t in range(TILES)]
+        low_first = keep.tile([P, 4, 2, DOCS], F32, name="low_first", tag="late1")
+        low_rest = keep.tile([P, 4, 2, DOCS], F32, name="low_rest")
+        low = {place: (low_first, low_rest)[i // 4][:, i % 4, :, :] for i, place in enumerate(ORDER)}
         y = [keep.tile([P, 2 * DOCS], F32, name="y%d" % t) for t in range(TILES)]
 
         def product(t, h):
-            acc = psum.tile([P, HALF], F32, name="acc%d_%d" % (t, h))
+            acc = psum.tile([P, HALF], F32, name="acc%d_%d" % (t, h), tag="acc%d_%d" % (t, h))
             nc.tensor.matmul_mx(
                 out=acc[:],
                 lhsT=w_codes[t][:].bitcast(FP8X4),
@@ -105,9 +116,8 @@ def tile_picked_ysplade_max_p_kernel(tc, x_words, x_scales, w1, bias, offs, out)
             )
             tokens = acc[:].rearrange("p (v d) -> p d v", d=D)
             b = b_col[:, t : t + 1]
-            low = keep.tile([P, 2, DOCS], F32, name="low%d_%d" % (t, h))
-            nc.scalar.activation(low[:], tokens[:, 0:2, :], ACT.Relu, bias=b)
-            nc.vector.scalar_tensor_tensor(pair[t][:, :, DOCS * h : DOCS * (h + 1)], tokens[:, 2:4, :], b, low[:], ALU.add, ALU.max)
+            nc.scalar.activation(low[t, h], tokens[:, 0:2, :], ACT.Relu, bias=b)
+            nc.vector.scalar_tensor_tensor(pair[t][:, :, DOCS * h : DOCS * (h + 1)], tokens[:, 2:4, :], b, low[t, h], ALU.add, ALU.max)
 
         def finish(t, docs):
             nc.vector.tensor_tensor(best[t][:, docs], pair[t][:, 0, docs], pair[t][:, 1, docs], ALU.max)

@@ -34,12 +34,11 @@ def tile_picked_ysplade_max_p_kernel(tc, x_words, x_scales, w1, bias, offs, out)
         keep = ctx.enter_context(tc.tile_pool(name="keep", bufs=1))
         psum = ctx.enter_context(tc.psum_pool(name="psum", bufs=1))
 
-        offsets = keep.tile([P, S // LIST_GROUP], U16, name="offsets")
-        nc.sync.dma_start(offsets[:], offs)
-
         w_rows = w1.rearrange("(p j) n -> p j n", j=PACK)
         w_early = keep.tile([P, PACK, 2 * P], F32, name="w_early")
         nc.sync.dma_start(w_early[:, :ROWS_AHEAD, :], w_rows[:, :ROWS_AHEAD, : 2 * P])
+        offsets = keep.tile([P, S // LIST_GROUP], U16, name="offsets")
+        nc.sync.dma_start(offsets[:], offs)
         w_late = [keep.tile([P, PACK, P], F32, name="w_late%d" % i, tag="late%d" % i) for i in range(2)]
         w_raw = [w_early[:, :, :P], w_early[:, :, P:], w_late[0][:], w_late[1][:]]
 
@@ -55,17 +54,18 @@ def tile_picked_ysplade_max_p_kernel(tc, x_words, x_scales, w1, bias, offs, out)
         nc.sync.dma_start(w_late[1][:], w_rows[:, :, 3 * P :])
 
         b_rows = keep.tile([P, P], F32, name="b_rows")
-        nc.gpsimd.memset(b_rows[:], 0.0)
+        nc.vector.memset(b_rows[:], 0.0)
         nc.scalar.dma_start(b_rows[:TILES, :], bias.rearrange("(t p) o -> t (p o)", p=P))
         identity = keep.tile([P, P], F32, name="identity")
-        make_identity(nc, identity[:])
+        nc.vector.memset(identity[:], 0.0)
+        make_identity(nc, identity[:], nomemset=True)
         b_turned = psum.tile([P, P], F32, name="b_turned", tag="acc%d_%d" % ORDER[-1])
         nc.tensor.transpose(b_turned[:], b_rows[:], identity[:])
         b_col = keep.tile([P, TILES], F32, name="b_col")
         nc.scalar.copy(b_col[:], b_turned[:, :TILES])
 
         one = keep.tile([P, 1], F32, name="one")
-        nc.gpsimd.memset(one[:], 1.0)
+        nc.vector.memset(one[:], 1.0)
         warm = keep.tile([P, 1], F32, name="warm")
         nc.scalar.activation(warm[:], one[:], ACT.Ln)
 

@@ -25,6 +25,7 @@ LIST_GROUP = 16
 QUADRANT = 32
 BLOCK_ROWS = 8
 ROWS_AHEAD = 3
+DIRECT = 2
 ORDER = [(0, 0), (1, 0), (0, 1), (1, 1), (2, 0), (2, 1), (3, 0), (3, 1)]
 
 
@@ -103,6 +104,8 @@ def tile_picked_ysplade_max_p_kernel(tc, x_words, x_scales, w1, bias, offs, out)
         low = {place: (low_first, low_rest)[i // 4][:, i % 4, :, :] for i, place in enumerate(ORDER)}
         y = [keep.tile([P, 2 * DOCS], F32, name="y%d" % t) for t in range(TILES)]
 
+        raw_best = keep.tile([P, DIRECT, DOCS], F32, name="raw_best")
+
         def product(t, h):
             acc = psum.tile([P, HALF], F32, name="acc%d_%d" % (t, h), tag="acc%d_%d" % (t, h))
             nc.tensor.matmul_mx(
@@ -114,13 +117,18 @@ def tile_picked_ysplade_max_p_kernel(tc, x_words, x_scales, w1, bias, offs, out)
                 start=True,
                 stop=True,
             )
-            tokens = acc[:].rearrange("p (v d) -> p d v", d=D)
             b = b_col[:, t : t + 1]
+            if (t, h) in ORDER[:DIRECT]:
+                nc.vector.tensor_reduce(raw_best[:, t, :], acc[:].rearrange("p (v d) -> p v d", d=D), mybir.AxisListType.X, ALU.max)
+                nc.scalar.activation(best[t][:, :DOCS], raw_best[:, t, :], ACT.Relu, bias=b)
+                return
+            tokens = acc[:].rearrange("p (v d) -> p d v", d=D)
             nc.scalar.activation(low[t, h], tokens[:, 0:2, :], ACT.Relu, bias=b)
             nc.vector.scalar_tensor_tensor(pair[t][:, :, DOCS * h : DOCS * (h + 1)], tokens[:, 2:4, :], b, low[t, h], ALU.add, ALU.max)
 
         def finish(t, docs):
-            nc.vector.tensor_tensor(best[t][:, docs], pair[t][:, 0, docs], pair[t][:, 1, docs], ALU.max)
+            paired = slice(DOCS, 2 * DOCS) if t < DIRECT else docs
+            nc.vector.tensor_tensor(best[t][:, paired], pair[t][:, 0, paired], pair[t][:, 1, paired], ALU.max)
             nc.scalar.activation(y[t][:, docs], best[t][:, docs], ACT.Ln, bias=1.0)
             nc.sync.dma_start(out[P * t : P * (t + 1), docs], y[t][:, docs])
 

@@ -24,7 +24,7 @@ TILES = N // P
 LIST_GROUP = 16
 QUADRANT = 32
 BLOCK_ROWS = 8
-ROWS_AHEAD = 3
+TABLE_ROW = 112
 DIRECT = 2
 ORDER = [(0, 0), (1, 0), (0, 1), (1, 1), (2, 0), (2, 1), (3, 0), (3, 1)]
 
@@ -37,16 +37,15 @@ def tile_picked_ysplade_max_p_kernel(tc, x_words, x_scales, w1, bias, offs, out)
 
         w_rows = w1.rearrange("(p j) n -> p j n", j=PACK)
         w_early = keep.tile([P, PACK, 2 * P], F32, name="w_early")
-        nc.sync.dma_start(w_early[:, :ROWS_AHEAD, :], w_rows[:, :ROWS_AHEAD, : 2 * P])
+        scale_table = keep.tile([P, T], U8, name="scale_table")
+        nc.sync.dma_start(scale_table[TABLE_ROW:, :].bitcast(I32), x_scales[0].bitcast(I32))
+        nc.vector.memset(scale_table[:TABLE_ROW, :].bitcast(I32), 0)
         offsets = keep.tile([P, S // LIST_GROUP], U16, name="offsets")
         nc.sync.dma_start(offsets[:], offs)
+        nc.sync.dma_start(w_early[:], w_rows[:, :, : 2 * P])
         w_late = [keep.tile([P, PACK, P], F32, name="w_late%d" % i, tag="late%d" % i) for i in range(2)]
         w_raw = [w_early[:, :, :P], w_early[:, :, P:], w_late[0][:], w_late[1][:]]
 
-        scale_table = keep.tile([P, T], U8, name="scale_table")
-        nc.vector.memset(scale_table[:].bitcast(I32), 0)
-        nc.sync.dma_start(scale_table[0:P:BLOCK_ROWS, :].bitcast(I32), x_scales[0].bitcast(I32))
-        nc.sync.dma_start(w_early[:, ROWS_AHEAD:, :], w_rows[:, ROWS_AHEAD:, : 2 * P])
 
         word_table = keep.tile([P, T], I32, name="word_table")
         nc.sync.dma_start(word_table[:], x_words[0].rearrange("p n t -> p (n t)").bitcast(I32))
@@ -73,9 +72,9 @@ def tile_picked_ysplade_max_p_kernel(tc, x_words, x_scales, w1, bias, offs, out)
         picked_sc = keep.tile([P, S], U8, name="picked_sc", align_bytes=64)
         nc.vector.tensor_copy(picked_sc[:], scale_table[:].indirect(offsets[:]))
         x_sc = keep.tile([P, S], U8, name="x_sc", align_bytes=64)
-        nc.vector.tensor_copy(x_sc[:].bitcast(I32), picked_sc[:].bitcast(I32))
-        for r in range(1, QUADRANT // BLOCK_ROWS):
-            nc.scalar.dma_start(x_sc[r:P:QUADRANT, :].bitcast(I32), picked_sc[BLOCK_ROWS * r : P : QUADRANT, :].bitcast(I32))
+        nc.vector.memset(x_sc[:].bitcast(I32), 0)
+        for q in range(P // QUADRANT):
+            nc.scalar.dma_start(x_sc[QUADRANT * q : QUADRANT * q + 4, :].bitcast(I32), picked_sc[TABLE_ROW + 4 * q : TABLE_ROW + 4 * q + 4, :].bitcast(I32))
 
         w_codes, w_sc = [], []
 

@@ -78,23 +78,30 @@ def tile_picked_ysplade_max_p_kernel(tc, x_words, x_scales, w1, bias, offs, out)
 
         w_codes, w_sc = [], []
 
-        def quantise(t):
+        rounded = []
+
+        def round_weights(t):
             grouped = keep.tile([P, P, PACK], BF16, name="grouped%d" % t, align_bytes=64)
             nc.scalar.copy(grouped[:].rearrange("p (c i) j -> p c j i", i=4), w_raw[t].rearrange("p j (c i) -> p c j i", i=4))
-            w_codes.append(keep.tile([P, P], U32, name="w_codes%d" % t, align_bytes=64))
-            w_sc.append(keep.tile([P, P], U8, name="w_sc%d" % t, align_bytes=64))
-            nc.vector.quantize_mx(out=w_codes[t][:].bitcast(FP8X4), scales=w_sc[t][:], in_=grouped[:].rearrange("p m j -> p (m j)"))
+            rounded.append(grouped)
 
-        quantise(0)
-        quantise(1)
+        def quantise(t):
+            w_codes.append(keep.tile([P, P], U32, name="w_codes%d" % t, align_bytes=64))
+            w_sc.append(keep.tile([P, P], U8, name="w_sc%d" % t, tag="w_sc%d" % t, align_bytes=64))
+            nc.vector.quantize_mx(out=w_codes[t][:].bitcast(FP8X4), scales=w_sc[t][:], in_=rounded[t][:].rearrange("p m j -> p (m j)"))
+
+        for t in range(2):
+            round_weights(t)
+            quantise(t)
 
         x_codes = [keep.tile([P, HALF], U32, name="x_codes%d" % h, align_bytes=64) for h in range(2)]
         for h in range(2):
             columns = slice(h * HALF // LIST_GROUP, (h + 1) * HALF // LIST_GROUP)
             nc.vector.tensor_copy(x_codes[h][:], word_table[:].bitcast(U32).indirect(offsets[:, columns]))
 
+        round_weights(2)
         quantise(2)
-        quantise(3)
+        round_weights(3)
 
         best = [keep.tile([P, 2 * DOCS], F32, name="best%d" % t) for t in range(TILES)]
         pair = [keep.tile([P, 2, 2 * DOCS], F32, name="pair%d" % t) for t in range(TILES)]
@@ -103,7 +110,7 @@ def tile_picked_ysplade_max_p_kernel(tc, x_words, x_scales, w1, bias, offs, out)
         low = {place: (low_first, low_rest)[i // 4][:, i % 4, :, :] for i, place in enumerate(ORDER)}
         y = [keep.tile([P, 2 * DOCS], F32, name="y%d" % t) for t in range(TILES)]
 
-        raw_best = keep.tile([P, DIRECT, DOCS], F32, name="raw_best")
+        raw_best = [keep.tile([P, DOCS], F32, name="raw_best%d" % t, tag=("w_sc3", "raw_best1")[t], align_bytes=64) for t in range(DIRECT)]
 
         def product(t, h):
             acc = psum.tile([P, HALF], F32, name="acc%d_%d" % (t, h), tag="acc%d_%d" % (t, h))
@@ -118,8 +125,8 @@ def tile_picked_ysplade_max_p_kernel(tc, x_words, x_scales, w1, bias, offs, out)
             )
             b = b_col[:, t : t + 1]
             if (t, h) in ORDER[:DIRECT]:
-                nc.vector.tensor_reduce(raw_best[:, t, :], acc[:].rearrange("p (v d) -> p v d", d=D), mybir.AxisListType.X, ALU.max)
-                nc.scalar.activation(best[t][:, :DOCS], raw_best[:, t, :], ACT.Relu, bias=b)
+                nc.vector.tensor_reduce(raw_best[t][:], acc[:].rearrange("p (v d) -> p v d", d=D), mybir.AxisListType.X, ALU.max)
+                nc.scalar.activation(best[t][:, :DOCS], raw_best[t][:], ACT.Relu, bias=b)
                 return
             tokens = acc[:].rearrange("p (v d) -> p d v", d=D)
             nc.scalar.activation(low[t, h], tokens[:, 0:2, :], ACT.Relu, bias=b)
@@ -134,6 +141,8 @@ def tile_picked_ysplade_max_p_kernel(tc, x_words, x_scales, w1, bias, offs, out)
         for step in range(len(ORDER) + 1):
             if step < len(ORDER):
                 product(*ORDER[step])
+            if step == DIRECT - 1:
+                quantise(TILES - 1)
             if step > 0:
                 t, h = ORDER[step - 1]
                 if t == TILES - 1:

@@ -26,6 +26,7 @@ QUADRANT = 32
 BLOCK_ROWS = 8
 TABLE_ROW = 112
 DIRECT = 2
+QUARTER = HALF // 2
 ORDER = [(0, 0), (1, 0), (0, 1), (1, 1), (2, 0), (2, 1), (3, 0), (3, 1)]
 
 
@@ -94,10 +95,10 @@ def tile_picked_ysplade_max_p_kernel(tc, x_words, x_scales, w1, bias, offs, out)
             round_weights(t)
             quantise(t)
 
-        x_codes = [keep.tile([P, HALF], U32, name="x_codes%d" % h, align_bytes=64) for h in range(2)]
-        for h in range(2):
-            columns = slice(h * HALF // LIST_GROUP, (h + 1) * HALF // LIST_GROUP)
-            nc.vector.tensor_copy(x_codes[h][:], word_table[:].bitcast(U32).indirect(offsets[:, columns]))
+        x_codes = [keep.tile([P, QUARTER], U32, name="x_codes%d" % q, align_bytes=64) for q in range(4)]
+        for q in range(4):
+            columns = slice(q * QUARTER // LIST_GROUP, (q + 1) * QUARTER // LIST_GROUP)
+            nc.vector.tensor_copy(x_codes[q][:], word_table[:].bitcast(U32).indirect(offsets[:, columns]))
 
         round_weights(2)
         quantise(2)
@@ -112,23 +113,36 @@ def tile_picked_ysplade_max_p_kernel(tc, x_words, x_scales, w1, bias, offs, out)
 
         raw_best = [keep.tile([P, DOCS], F32, name="raw_best%d" % t, tag=("w_sc3", "raw_best1")[t], align_bytes=64) for t in range(DIRECT)]
 
-        def product(t, h):
-            acc = psum.tile([P, HALF], F32, name="acc%d_%d" % (t, h), tag="acc%d_%d" % (t, h))
+        acc = {}
+
+        def one_pass(t, q):
+            if q % 2 == 0:
+                acc[t, q // 2] = psum.tile([P, HALF], F32, name="acc%d_%d" % (t, q // 2), tag="acc%d_%d" % (t, q // 2))
             nc.tensor.matmul_mx(
-                out=acc[:],
+                out=acc[t, q // 2][:, QUARTER * (q % 2) : QUARTER * (q % 2 + 1)],
                 lhsT=w_codes[t][:].bitcast(FP8X4),
                 lhsT_scale=w_sc[t][:],
-                rhs=x_codes[h][:].bitcast(FP8X4),
-                rhs_scale=x_sc[:, HALF * h : HALF * (h + 1)],
+                rhs=x_codes[q][:].bitcast(FP8X4),
+                rhs_scale=x_sc[:, QUARTER * q : QUARTER * (q + 1)],
                 start=True,
                 stop=True,
             )
+
+        for q in range(4):
+            for t in range(2):
+                one_pass(t, q)
+
+        def product(t, h):
+            if t >= 2:
+                one_pass(t, 2 * h)
+                one_pass(t, 2 * h + 1)
+            bank = acc[t, h]
             b = b_col[:, t : t + 1]
             if (t, h) in ORDER[:DIRECT]:
-                nc.vector.tensor_reduce(raw_best[t][:], acc[:].rearrange("p (v d) -> p v d", d=D), mybir.AxisListType.X, ALU.max)
+                nc.vector.tensor_reduce(raw_best[t][:], bank[:].rearrange("p (v d) -> p v d", d=D), mybir.AxisListType.X, ALU.max)
                 nc.scalar.activation(best[t][:, :DOCS], raw_best[t][:], ACT.Relu, bias=b)
                 return
-            tokens = acc[:].rearrange("p (v d) -> p d v", d=D)
+            tokens = bank[:].rearrange("p (v d) -> p d v", d=D)
             nc.scalar.activation(low[t, h], tokens[:, 0:2, :], ACT.Relu, bias=b)
             nc.vector.scalar_tensor_tensor(pair[t][:, :, DOCS * h : DOCS * (h + 1)], tokens[:, 2:4, :], b, low[t, h], ALU.add, ALU.max)
 

@@ -146,20 +146,35 @@ def tile_picked_ysplade_max_p_kernel(tc, x_words, x_scales, w1, bias, offs, out)
             nc.scalar.activation(low[t, h], tokens[:, 0:2, :], ACT.Relu, bias=b)
             nc.vector.scalar_tensor_tensor(pair[t][:, :, DOCS * h : DOCS * (h + 1)], tokens[:, 2:4, :], b, low[t, h], ALU.add, ALU.max)
 
-        def finish(t, docs):
-            paired = slice(DOCS, 2 * DOCS) if t < DIRECT else docs
-            nc.vector.tensor_tensor(best[t][:, paired], pair[t][:, 0, paired], pair[t][:, 1, paired], ALU.max)
-            nc.scalar.activation(y[t][:, docs], best[t][:, docs], ACT.Ln, bias=1.0)
-            nc.sync.dma_start(out[P * t : P * (t + 1), docs], y[t][:, docs])
+        def largest(t, docs):
+            nc.vector.tensor_tensor(best[t][:, docs], pair[t][:, 0, docs], pair[t][:, 1, docs], ALU.max)
 
-        for step in range(len(ORDER) + 1):
-            if step < len(ORDER):
-                product(*ORDER[step])
-            if step == DIRECT - 1:
-                quantise(TILES - 1)
-            if step > 0:
-                t, h = ORDER[step - 1]
-                if t == TILES - 1:
-                    finish(t, slice(DOCS * h, DOCS * (h + 1)))
-                elif h == 1:
-                    finish(t, slice(0, 2 * DOCS))
+        def log_of(t, docs):
+            nc.scalar.activation(y[t][:, docs], best[t][:, docs], ACT.Ln, bias=1.0)
+
+        def store(t):
+            nc.sync.dma_start(out[P * t : P * (t + 1), :], y[t][:])
+
+        both, halves = slice(0, 2 * DOCS), [slice(0, DOCS), slice(DOCS, 2 * DOCS)]
+        for t in range(DIRECT):
+            product(t, 0)
+        quantise(TILES - 1)
+        for t in range(DIRECT):
+            product(t, 1)
+        for t in range(DIRECT):
+            largest(t, halves[1])
+        product(2, 0)
+        product(2, 1)
+        log_of(0, both)
+        store(0)
+        largest(2, halves[0])
+        product(3, 0)
+        largest(2, halves[1])
+        product(3, 1)
+        for t in (1, 2):
+            log_of(t, both)
+            store(t)
+        for docs in halves:
+            largest(3, docs)
+            log_of(3, docs)
+        store(3)

@@ -152,8 +152,8 @@ def tile_picked_ysplade_max_p_kernel(tc, x_words, x_scales, w1, bias, offs, out)
         def log_of(t, docs):
             nc.scalar.activation(y[t][:, docs], best[t][:, docs], ACT.Ln, bias=1.0)
 
-        def store(t):
-            nc.sync.dma_start(out[P * t : P * (t + 1), :], y[t][:])
+        def store(t, docs):
+            nc.sync.dma_start(out[P * t : P * (t + 1), docs], y[t][:, docs])
 
         both, halves = slice(0, 2 * DOCS), [slice(0, DOCS), slice(DOCS, 2 * DOCS)]
         for t in range(DIRECT):
@@ -166,15 +166,15 @@ def tile_picked_ysplade_max_p_kernel(tc, x_words, x_scales, w1, bias, offs, out)
         product(2, 0)
         product(2, 1)
         log_of(0, both)
-        store(0)
+        store(0, both)
         largest(2, halves[0])
         product(3, 0)
         largest(2, halves[1])
         product(3, 1)
         for t in (1, 2):
             log_of(t, both)
-            store(t)
+            store(t, both)
         for docs in halves:
             largest(3, docs)
             log_of(3, docs)
-        store(3)
+            store(3, docs)

@@ -25,45 +25,42 @@ LIST_GROUP = 16
 QUADRANT = 32
 BLOCK_ROWS = 8
 TABLE_ROW = 112
-DIRECT = 2
+LARGEST = 3.4028234663852886e38
 QUARTER = HALF // 2
-ORDER = [(0, 0), (1, 0), (0, 1), (1, 1), (2, 0), (2, 1), (3, 0), (3, 1)]
 
 
 def tile_picked_ysplade_max_p_kernel(tc, x_words, x_scales, w1, bias, offs, out):
     nc = tc.nc
     with ExitStack() as ctx:
         keep = ctx.enter_context(tc.tile_pool(name="keep", bufs=1))
+        placed = ctx.enter_context(tc.tile_pool(name="placed", bufs=1))
         psum = ctx.enter_context(tc.psum_pool(name="psum", bufs=1))
 
-        w_rows = w1.rearrange("(p j) n -> p j n", j=PACK)
-        w_early = keep.tile([P, PACK, 2 * P], F32, name="w_early")
         scale_table = keep.tile([P, T], U8, name="scale_table")
         nc.sync.dma_start(scale_table[TABLE_ROW:, :].bitcast(I32), x_scales[0].bitcast(I32))
         nc.vector.memset(scale_table[:TABLE_ROW, :].bitcast(I32), 0)
         offsets = keep.tile([P, S // LIST_GROUP], U16, name="offsets")
         nc.sync.dma_start(offsets[:], offs)
-        nc.sync.dma_start(w_early[:], w_rows[:, :, : 2 * P])
-        w_late = [keep.tile([P, PACK, P], F32, name="w_late%d" % i, tag="late%d" % i) for i in range(2)]
-        w_raw = [w_early[:, :, :P], w_early[:, :, P:], w_late[0][:], w_late[1][:]]
-
-
-        word_table = keep.tile([P, T], I32, name="word_table")
+        word_table = keep.tile([P, T], I32, name="word_table", tag="words", align_bytes=64)
         nc.sync.dma_start(word_table[:], x_words[0].rearrange("p n t -> p (n t)").bitcast(I32))
-
-        nc.sync.dma_start(w_late[0][:], w_rows[:, :, 2 * P : 3 * P])
-        nc.sync.dma_start(w_late[1][:], w_rows[:, :, 3 * P :])
+        w_rows = w1.rearrange("(p j) n -> p j n", j=PACK)
+        w_one = [keep.tile([P, PACK, P], F32, name="w_one%d" % i, tag="w_one%d" % i) for i in range(2)]
+        for i in range(2):
+            nc.sync.dma_start(w_one[i][:], w_rows[:, :, i * P : (i + 1) * P])
+        w_two = placed.tile([P, PACK, 2 * P], F32, name="w_two", offset=0, align_bytes=64)
+        nc.sync.dma_start(w_two[:], w_rows[:, :, 2 * P :])
+        w_raw = [w_one[0][:], w_one[1][:], w_two[:, :, :P], w_two[:, :, P:]]
 
         b_rows = keep.tile([P, P], F32, name="b_rows")
-        nc.vector.memset(b_rows[:], 0.0)
-        nc.scalar.dma_start(b_rows[:TILES, :], bias.rearrange("(t p) o -> t (p o)", p=P))
+        nc.scalar.dma_start(b_rows[P - TILES :, :], bias.rearrange("(t p) o -> t (p o)", p=P))
+        nc.vector.memset(b_rows[: P - TILES, :], 0.0)
         identity = keep.tile([P, P], F32, name="identity")
         nc.vector.memset(identity[:], 0.0)
         make_identity(nc, identity[:], nomemset=True)
-        b_turned = psum.tile([P, P], F32, name="b_turned", tag="acc%d_%d" % ORDER[-1])
+        b_turned = psum.tile([P, P], F32, name="b_turned", tag="acc3_1")
         nc.tensor.transpose(b_turned[:], b_rows[:], identity[:])
         b_col = keep.tile([P, TILES], F32, name="b_col")
-        nc.scalar.copy(b_col[:], b_turned[:, :TILES])
+        nc.scalar.copy(b_col[:], b_turned[:, P - TILES :])
 
         one = keep.tile([P, 1], F32, name="one")
         nc.vector.memset(one[:], 1.0)
@@ -77,103 +74,104 @@ def tile_picked_ysplade_max_p_kernel(tc, x_words, x_scales, w1, bias, offs, out)
         for q in range(P // QUADRANT):
             nc.scalar.dma_start(x_sc[QUADRANT * q : QUADRANT * q + 4, :].bitcast(I32), picked_sc[TABLE_ROW + 4 * q : TABLE_ROW + 4 * q + 4, :].bitcast(I32))
 
-        w_codes, w_sc = [], []
+        b_neg = keep.tile([P, 2], F32, name="b_neg")
+        nc.scalar.mul(b_neg[:], b_col[:, :2], -1.0)
+        b_one = keep.tile([P, 2], F32, name="b_one")
+        nc.scalar.add(b_one[:], b_col[:, :2], 1.0)
 
-        rounded = []
+        x_codes, rounded, w_codes, w_sc, acc, low, raw = {}, {}, {}, {}, {}, {}, {}
 
-        def round_weights(t):
-            grouped = keep.tile([P, P, PACK], BF16, name="grouped%d" % t, align_bytes=64)
-            nc.scalar.copy(grouped[:].rearrange("p (c i) j -> p c j i", i=4), w_raw[t].rearrange("p j (c i) -> p c j i", i=4))
-            rounded.append(grouped)
-
-        def quantise(t):
-            w_codes.append(keep.tile([P, P], U32, name="w_codes%d" % t, align_bytes=64))
-            w_sc.append(keep.tile([P, P], U8, name="w_sc%d" % t, tag="w_sc%d" % t, align_bytes=64))
-            nc.vector.quantize_mx(out=w_codes[t][:].bitcast(FP8X4), scales=w_sc[t][:], in_=rounded[t][:].rearrange("p m j -> p (m j)"))
-
-        for t in range(2):
-            round_weights(t)
-            quantise(t)
-
-        x_codes = [keep.tile([P, QUARTER], U32, name="x_codes%d" % q, align_bytes=64) for q in range(4)]
-        for q in range(4):
+        def gather(q):
+            x_codes[q] = keep.tile([P, QUARTER], U32, name="x_codes%d" % q, tag="grouped0" if q == 3 else "x_codes%d" % q, align_bytes=64)
             columns = slice(q * QUARTER // LIST_GROUP, (q + 1) * QUARTER // LIST_GROUP)
             nc.vector.tensor_copy(x_codes[q][:], word_table[:].bitcast(U32).indirect(offsets[:, columns]))
 
-        round_weights(2)
-        quantise(2)
-        round_weights(3)
+        def round_weights(t):
+            rounded[t] = keep.tile([P, P, PACK], BF16, name="grouped%d" % t, tag="grouped%d" % t, align_bytes=64)
+            nc.scalar.copy(rounded[t][:].rearrange("p (c i) j -> p c j i", i=4), w_raw[t].rearrange("p j (c i) -> p c j i", i=4))
+
+        def quantise(t):
+            w_codes[t] = keep.tile([P, P], U32, name="w_codes%d" % t, tag=("w_codes0", "words")[t % 2], align_bytes=64)
+            w_sc[t] = keep.tile([P, P], U8, name="w_sc%d" % t, align_bytes=64)
+            nc.vector.quantize_mx(out=w_codes[t][:].bitcast(FP8X4), scales=w_sc[t][:], in_=rounded[t][:].rearrange("p m j -> p (m j)"))
 
         best = [keep.tile([P, 2 * DOCS], F32, name="best%d" % t) for t in range(TILES)]
-        pair = [keep.tile([P, 2, 2 * DOCS], F32, name="pair%d" % t) for t in range(TILES)]
-        low_first = keep.tile([P, 4, 2, DOCS], F32, name="low_first", tag="late1")
-        low_rest = keep.tile([P, 4, 2, DOCS], F32, name="low_rest")
-        low = {place: (low_first, low_rest)[i // 4][:, i % 4, :, :] for i, place in enumerate(ORDER)}
+        pair = {t: keep.tile([P, 2, 2 * DOCS], F32, name="pair%d" % t) for t in range(2, TILES)}
         y = [keep.tile([P, 2 * DOCS], F32, name="y%d" % t) for t in range(TILES)]
+        both, halves = slice(0, 2 * DOCS), [slice(0, DOCS), slice(DOCS, 2 * DOCS)]
 
-        raw_best = [keep.tile([P, DOCS], F32, name="raw_best%d" % t, tag=("w_sc3", "raw_best1")[t], align_bytes=64) for t in range(DIRECT)]
+        def multiply(t, h):
+            acc[t, h] = psum.tile([P, HALF], F32, name="acc%d_%d" % (t, h), tag="acc%d_%d" % (t, h))
+            for q in (2 * h, 2 * h + 1):
+                nc.tensor.matmul_mx(
+                    out=acc[t, h][:, QUARTER * (q % 2) : QUARTER * (q % 2 + 1)],
+                    lhsT=w_codes[t][:].bitcast(FP8X4),
+                    lhsT_scale=w_sc[t][:],
+                    rhs=x_codes[q][:].bitcast(FP8X4),
+                    rhs_scale=x_sc[:, QUARTER * q : QUARTER * (q + 1)],
+                    start=True,
+                    stop=True,
+                )
 
-        acc = {}
+        def reduce_whole(t, h):
+            raw[t, h] = keep.tile([P, DOCS], F32, name="raw%d_%d" % (t, h), tag="grouped%d" % (2 + h) if t == 1 else "raw%d" % h, align_bytes=64)
+            nc.vector.tensor_reduce(raw[t, h][:], acc[t, h][:].rearrange("p (v d) -> p v d", d=D), mybir.AxisListType.X, ALU.max)
+            nc.gpsimd.tensor_scalar(best[t][:, halves[h]], raw[t, h][:], LARGEST, b_neg[:, t : t + 1], ALU.min, ALU.max)
 
-        def one_pass(t, q):
-            if q % 2 == 0:
-                acc[t, q // 2] = psum.tile([P, HALF], F32, name="acc%d_%d" % (t, q // 2), tag="acc%d_%d" % (t, q // 2))
-            nc.tensor.matmul_mx(
-                out=acc[t, q // 2][:, QUARTER * (q % 2) : QUARTER * (q % 2 + 1)],
-                lhsT=w_codes[t][:].bitcast(FP8X4),
-                lhsT_scale=w_sc[t][:],
-                rhs=x_codes[q][:].bitcast(FP8X4),
-                rhs_scale=x_sc[:, QUARTER * q : QUARTER * (q + 1)],
-                start=True,
-                stop=True,
-            )
+        def relu_low(t, h):
+            low[t, h] = keep.tile([P, 2, DOCS], F32, name="low%d_%d" % (t, h))
+            nc.scalar.activation(low[t, h][:], acc[t, h][:].rearrange("p (v d) -> p d v", d=D)[:, 0:2, :], ACT.Relu, bias=b_col[:, t : t + 1])
 
-        for q in range(4):
-            for t in range(2):
-                one_pass(t, q)
-
-        def product(t, h):
-            if t >= 2:
-                one_pass(t, 2 * h)
-                one_pass(t, 2 * h + 1)
-            bank = acc[t, h]
-            b = b_col[:, t : t + 1]
-            if (t, h) in ORDER[:DIRECT]:
-                nc.vector.tensor_reduce(raw_best[t][:], bank[:].rearrange("p (v d) -> p v d", d=D), mybir.AxisListType.X, ALU.max)
-                nc.scalar.activation(best[t][:, :DOCS], raw_best[t][:], ACT.Relu, bias=b)
-                return
-            tokens = bank[:].rearrange("p (v d) -> p d v", d=D)
-            nc.scalar.activation(low[t, h], tokens[:, 0:2, :], ACT.Relu, bias=b)
-            nc.vector.scalar_tensor_tensor(pair[t][:, :, DOCS * h : DOCS * (h + 1)], tokens[:, 2:4, :], b, low[t, h], ALU.add, ALU.max)
+        def pairs(t, h):
+            tokens = acc[t, h][:].rearrange("p (v d) -> p d v", d=D)
+            nc.vector.scalar_tensor_tensor(pair[t][:, :, halves[h]], tokens[:, 2:4, :], b_col[:, t : t + 1], low[t, h][:], ALU.add, ALU.max)
 
         def largest(t, docs):
             nc.vector.tensor_tensor(best[t][:, docs], pair[t][:, 0, docs], pair[t][:, 1, docs], ALU.max)
 
         def log_of(t, docs):
-            nc.scalar.activation(y[t][:, docs], best[t][:, docs], ACT.Ln, bias=1.0)
+            nc.scalar.activation(y[t][:, docs], best[t][:, docs], ACT.Ln, bias=b_one[:, t : t + 1] if t < 2 else 1.0)
 
         def store(t, docs):
             nc.sync.dma_start(out[P * t : P * (t + 1), docs], y[t][:, docs])
 
-        both, halves = slice(0, 2 * DOCS), [slice(0, DOCS), slice(DOCS, 2 * DOCS)]
-        for t in range(DIRECT):
-            product(t, 0)
-        quantise(TILES - 1)
-        for t in range(DIRECT):
-            product(t, 1)
-        for t in range(DIRECT):
-            largest(t, halves[1])
-        product(2, 0)
-        product(2, 1)
+        for q in range(3):
+            gather(q)
+        round_weights(0)
+        quantise(0)
+        gather(3)
+        round_weights(1)
+        quantise(1)
+        round_weights(2)
+        round_weights(3)
+        for t in range(2):
+            multiply(t, 0)
+            multiply(t, 1)
+        reduce_whole(0, 0)
+        reduce_whole(0, 1)
+        quantise(2)
+        multiply(2, 0)
+        multiply(2, 1)
+        reduce_whole(1, 0)
+        quantise(3)
+        multiply(3, 0)
+        multiply(3, 1)
+        reduce_whole(1, 1)
         log_of(0, both)
         store(0, both)
-        largest(2, halves[0])
-        product(3, 0)
-        largest(2, halves[1])
-        product(3, 1)
-        for t in (1, 2):
-            log_of(t, both)
-            store(t, both)
+        relu_low(2, 0)
+        pairs(2, 0)
+        relu_low(2, 1)
+        pairs(2, 1)
+        log_of(1, both)
+        store(1, both)
+        relu_low(3, 0)
+        pairs(3, 0)
+        largest(2, both)
+        relu_low(3, 1)
+        pairs(3, 1)
+        log_of(2, both)
+        store(2, both)
         for docs in halves:
             largest(3, docs)
             log_of(3, docs)

@@ -36,23 +36,19 @@ def tile_picked_ysplade_max_p_kernel(tc, x_words, x_scales, w1, bias, offs, out)
         placed = ctx.enter_context(tc.tile_pool(name="placed", bufs=1))
         psum = ctx.enter_context(tc.psum_pool(name="psum", bufs=1))
 
-        scale_table = keep.tile([P, T], U8, name="scale_table")
+        scale_table = placed.tile([P, T], U8, name="scale_table", offset=0, align_bytes=64)
         nc.sync.dma_start(scale_table[TABLE_ROW:, :].bitcast(I32), x_scales[0].bitcast(I32))
         nc.vector.memset(scale_table[:TABLE_ROW, :].bitcast(I32), 0)
         offsets = keep.tile([P, S // LIST_GROUP], U16, name="offsets")
         nc.sync.dma_start(offsets[:], offs)
+        b_rows = keep.tile([P, P], F32, name="b_rows")
+        nc.scalar.dma_start(b_rows[P - TILES :, :], bias.rearrange("(t p) o -> t (p o)", p=P))
         word_table = keep.tile([P, T], I32, name="word_table", tag="words", align_bytes=64)
         nc.sync.dma_start(word_table[:], x_words[0].rearrange("p n t -> p (n t)").bitcast(I32))
         w_rows = w1.rearrange("(p j) n -> p j n", j=PACK)
-        w_one = [keep.tile([P, PACK, P], F32, name="w_one%d" % i, tag="w_one%d" % i) for i in range(2)]
-        for i in range(2):
-            nc.sync.dma_start(w_one[i][:], w_rows[:, :, i * P : (i + 1) * P])
-        w_two = placed.tile([P, PACK, 2 * P], F32, name="w_two", offset=0, align_bytes=64)
-        nc.sync.dma_start(w_two[:], w_rows[:, :, 2 * P :])
-        w_raw = [w_one[0][:], w_one[1][:], w_two[:, :, :P], w_two[:, :, P:]]
+        w_first = keep.tile([P, PACK, P], F32, name="w_first")
+        nc.sync.dma_start(w_first[:], w_rows[:, :, :P])
 
-        b_rows = keep.tile([P, P], F32, name="b_rows")
-        nc.scalar.dma_start(b_rows[P - TILES :, :], bias.rearrange("(t p) o -> t (p o)", p=P))
         nc.vector.memset(b_rows[: P - TILES, :], 0.0)
         identity = keep.tile([P, P], F32, name="identity")
         nc.vector.memset(identity[:], 0.0)
@@ -72,7 +68,12 @@ def tile_picked_ysplade_max_p_kernel(tc, x_words, x_scales, w1, bias, offs, out)
         x_sc = keep.tile([P, S], U8, name="x_sc", align_bytes=64)
         nc.vector.memset(x_sc[:].bitcast(I32), 0)
         for q in range(P // QUADRANT):
-            nc.scalar.dma_start(x_sc[QUADRANT * q : QUADRANT * q + 4, :].bitcast(I32), picked_sc[TABLE_ROW + 4 * q : TABLE_ROW + 4 * q + 4, :].bitcast(I32))
+            nc.sync.dma_start(x_sc[QUADRANT * q : QUADRANT * q + 4, :].bitcast(I32), picked_sc[TABLE_ROW + 4 * q : TABLE_ROW + 4 * q + 4, :].bitcast(I32))
+        w_second = placed.tile([P, PACK, P], F32, name="w_second", offset=0, align_bytes=64)
+        nc.sync.dma_start(w_second[:], w_rows[:, :, P : 2 * P])
+        w_two = placed.tile([P, PACK, 2 * P], F32, name="w_two", offset=2048, align_bytes=64)
+        nc.sync.dma_start(w_two[:], w_rows[:, :, 2 * P :])
+        w_raw = [w_first[:], w_second[:], w_two[:, :, :P], w_two[:, :, P:]]
 
         b_neg = keep.tile([P, 2], F32, name="b_neg")
         nc.scalar.mul(b_neg[:], b_col[:, :2], -1.0)
@@ -97,7 +98,7 @@ def tile_picked_ysplade_max_p_kernel(tc, x_words, x_scales, w1, bias, offs, out)
 
         best = [keep.tile([P, 2 * DOCS], F32, name="best%d" % t) for t in range(TILES)]
         pair = {t: keep.tile([P, 2, 2 * DOCS], F32, name="pair%d" % t) for t in range(2, TILES)}
-        y = [keep.tile([P, 2 * DOCS], F32, name="y%d" % t) for t in range(TILES)]
+        y = [placed.tile([P, 2 * DOCS], F32, name="y%d" % t, offset=2048 + 1024 * t, align_bytes=64) for t in range(TILES)]
         both, halves = slice(0, 2 * DOCS), [slice(0, DOCS), slice(DOCS, 2 * DOCS)]
 
         def multiply(t, h):
@@ -114,7 +115,10 @@ def tile_picked_ysplade_max_p_kernel(tc, x_words, x_scales, w1, bias, offs, out)
                 )
 
         def reduce_whole(t, h):
-            raw[t, h] = keep.tile([P, DOCS], F32, name="raw%d_%d" % (t, h), tag="grouped%d" % (2 + h) if t == 1 else "raw%d" % h, align_bytes=64)
+            if t == 0:
+                raw[t, h] = placed.tile([P, DOCS], F32, name="raw0_%d" % h, offset=512 * h, align_bytes=64)
+            else:
+                raw[t, h] = keep.tile([P, DOCS], F32, name="raw1_%d" % h, tag="grouped%d" % (2 + h), align_bytes=64)
             nc.vector.tensor_reduce(raw[t, h][:], acc[t, h][:].rearrange("p (v d) -> p v d", d=D), mybir.AxisListType.X, ALU.max)
             nc.gpsimd.tensor_scalar(best[t][:, halves[h]], raw[t, h][:], LARGEST, b_neg[:, t : t + 1], ALU.min, ALU.max)
 

@@ -46,7 +46,7 @@ def tile_picked_ysplade_max_p_kernel(tc, x_words, x_scales, w1, bias, offs, out)
         word_table = keep.tile([P, T], I32, name="word_table", tag="words", align_bytes=64)
         nc.sync.dma_start(word_table[:], x_words[0].rearrange("p n t -> p (n t)").bitcast(I32))
         w_rows = w1.rearrange("(p j) n -> p j n", j=PACK)
-        w_first = keep.tile([P, PACK, P], F32, name="w_first")
+        w_first = keep.tile([P, PACK, P], F32, name="w_first", tag="w_first", align_bytes=64)
         nc.sync.dma_start(w_first[:], w_rows[:, :, :P])
 
         nc.vector.memset(b_rows[: P - TILES, :], 0.0)
@@ -75,15 +75,20 @@ def tile_picked_ysplade_max_p_kernel(tc, x_words, x_scales, w1, bias, offs, out)
         nc.sync.dma_start(w_two[:], w_rows[:, :, 2 * P :])
         w_raw = [w_first[:], w_second[:], w_two[:, :, :P], w_two[:, :, P:]]
 
-        b_neg = keep.tile([P, 2], F32, name="b_neg")
-        nc.scalar.mul(b_neg[:], b_col[:, :2], -1.0)
-        b_one = keep.tile([P, 2], F32, name="b_one")
-        nc.scalar.add(b_one[:], b_col[:, :2], 1.0)
+        b_neg = keep.tile([P, 1], F32, name="b_neg")
+        nc.scalar.mul(b_neg[:], b_col[:, :1], -1.0)
+        b_one = keep.tile([P, 1], F32, name="b_one")
+        nc.scalar.add(b_one[:], b_col[:, :1], 1.0)
 
         x_codes, rounded, w_codes, w_sc, acc, low, raw = {}, {}, {}, {}, {}, {}, {}
 
         def gather(q):
-            x_codes[q] = keep.tile([P, QUARTER], U32, name="x_codes%d" % q, tag="grouped0" if q == 3 else "x_codes%d" % q, align_bytes=64)
+            if q == 2:
+                x_codes[q] = keep.tile([P, QUARTER], U32, name="x_codes2", tag="w_first", align_bytes=64)
+            elif q == 3:
+                x_codes[q] = placed.tile([P, QUARTER], U32, name="x_codes3", offset=0, align_bytes=64)
+            else:
+                x_codes[q] = keep.tile([P, QUARTER], U32, name="x_codes%d" % q, align_bytes=64)
             columns = slice(q * QUARTER // LIST_GROUP, (q + 1) * QUARTER // LIST_GROUP)
             nc.vector.tensor_copy(x_codes[q][:], word_table[:].bitcast(U32).indirect(offsets[:, columns]))
 
@@ -92,90 +97,84 @@ def tile_picked_ysplade_max_p_kernel(tc, x_words, x_scales, w1, bias, offs, out)
             nc.scalar.copy(rounded[t][:].rearrange("p (c i) j -> p c j i", i=4), w_raw[t].rearrange("p j (c i) -> p c j i", i=4))
 
         def quantise(t):
-            w_codes[t] = keep.tile([P, P], U32, name="w_codes%d" % t, tag=("w_codes0", "words")[t % 2], align_bytes=64)
+            w_codes[t] = keep.tile([P, P], U32, name="w_codes%d" % t, align_bytes=64)
             w_sc[t] = keep.tile([P, P], U8, name="w_sc%d" % t, align_bytes=64)
             nc.vector.quantize_mx(out=w_codes[t][:].bitcast(FP8X4), scales=w_sc[t][:], in_=rounded[t][:].rearrange("p m j -> p (m j)"))
 
+        def one_pass(t, q):
+            if q % 2 == 0:
+                acc[t, q // 2] = psum.tile([P, HALF], F32, name="acc%d_%d" % (t, q // 2), tag="acc%d_%d" % (t, q // 2))
+            nc.tensor.matmul_mx(
+                out=acc[t, q // 2][:, QUARTER * (q % 2) : QUARTER * (q % 2 + 1)],
+                lhsT=w_codes[t][:].bitcast(FP8X4),
+                lhsT_scale=w_sc[t][:],
+                rhs=x_codes[q][:].bitcast(FP8X4),
+                rhs_scale=x_sc[:, QUARTER * q : QUARTER * (q + 1)],
+                start=True,
+                stop=True,
+            )
+
+        gather(0)
+        gather(1)
+        for t in range(2):
+            round_weights(t)
+            quantise(t)
+            gather(2 + t)
+        for t, q in [(0, 0), (0, 1), (0, 2), (1, 0), (1, 1), (0, 3), (1, 2), (1, 3)]:
+            one_pass(t, q)
+        round_weights(2)
+        round_weights(3)
+
         best = [keep.tile([P, 2 * DOCS], F32, name="best%d" % t) for t in range(TILES)]
-        pair = {t: keep.tile([P, 2, 2 * DOCS], F32, name="pair%d" % t) for t in range(2, TILES)}
-        y = [placed.tile([P, 2 * DOCS], F32, name="y%d" % t, offset=2048 + 1024 * t, align_bytes=64) for t in range(TILES)]
+        pair = {t: keep.tile([P, 2, 2 * DOCS], F32, name="pair%d" % t) for t in range(1, TILES)}
+        low_all = placed.tile([P, 6, 2, DOCS], F32, name="low_all", offset=4096, align_bytes=64)
+        y = [keep.tile([P, 2 * DOCS], F32, name="y%d" % t) for t in range(TILES)]
         both, halves = slice(0, 2 * DOCS), [slice(0, DOCS), slice(DOCS, 2 * DOCS)]
 
-        def multiply(t, h):
-            acc[t, h] = psum.tile([P, HALF], F32, name="acc%d_%d" % (t, h), tag="acc%d_%d" % (t, h))
-            for q in (2 * h, 2 * h + 1):
-                nc.tensor.matmul_mx(
-                    out=acc[t, h][:, QUARTER * (q % 2) : QUARTER * (q % 2 + 1)],
-                    lhsT=w_codes[t][:].bitcast(FP8X4),
-                    lhsT_scale=w_sc[t][:],
-                    rhs=x_codes[q][:].bitcast(FP8X4),
-                    rhs_scale=x_sc[:, QUARTER * q : QUARTER * (q + 1)],
-                    start=True,
-                    stop=True,
-                )
-
-        def reduce_whole(t, h):
-            if t == 0:
-                raw[t, h] = placed.tile([P, DOCS], F32, name="raw0_%d" % h, offset=512 * h, align_bytes=64)
+        def reduce_whole(h):
+            if h == 0:
+                raw[h] = placed.tile([P, DOCS], F32, name="raw0", offset=1024, align_bytes=64)
             else:
-                raw[t, h] = keep.tile([P, DOCS], F32, name="raw1_%d" % h, tag="grouped%d" % (2 + h), align_bytes=64)
-            nc.vector.tensor_reduce(raw[t, h][:], acc[t, h][:].rearrange("p (v d) -> p v d", d=D), mybir.AxisListType.X, ALU.max)
-            nc.gpsimd.tensor_scalar(best[t][:, halves[h]], raw[t, h][:], LARGEST, b_neg[:, t : t + 1], ALU.min, ALU.max)
-
-        def relu_low(t, h):
-            low[t, h] = keep.tile([P, 2, DOCS], F32, name="low%d_%d" % (t, h))
-            nc.scalar.activation(low[t, h][:], acc[t, h][:].rearrange("p (v d) -> p d v", d=D)[:, 0:2, :], ACT.Relu, bias=b_col[:, t : t + 1])
+                raw[h] = keep.tile([P, DOCS], F32, name="raw1", tag="grouped2", align_bytes=64)
+            nc.vector.tensor_reduce(raw[h][:], acc[0, h][:].rearrange("p (v d) -> p v d", d=D), mybir.AxisListType.X, ALU.max)
+            nc.gpsimd.tensor_scalar(best[0][:, halves[h]], raw[h][:], LARGEST, b_neg[:], ALU.min, ALU.max)
 
         def pairs(t, h):
             tokens = acc[t, h][:].rearrange("p (v d) -> p d v", d=D)
-            nc.vector.scalar_tensor_tensor(pair[t][:, :, halves[h]], tokens[:, 2:4, :], b_col[:, t : t + 1], low[t, h][:], ALU.add, ALU.max)
+            b = b_col[:, t : t + 1]
+            low = low_all[:, 2 * (t - 1) + h, :, :]
+            nc.scalar.activation(low, tokens[:, 0:2, :], ACT.Relu, bias=b)
+            nc.vector.scalar_tensor_tensor(pair[t][:, :, halves[h]], tokens[:, 2:4, :], b, low, ALU.add, ALU.max)
 
         def largest(t, docs):
             nc.vector.tensor_tensor(best[t][:, docs], pair[t][:, 0, docs], pair[t][:, 1, docs], ALU.max)
 
         def log_of(t, docs):
-            nc.scalar.activation(y[t][:, docs], best[t][:, docs], ACT.Ln, bias=b_one[:, t : t + 1] if t < 2 else 1.0)
+            nc.scalar.activation(y[t][:, docs], best[t][:, docs], ACT.Ln, bias=b_one[:] if t == 0 else 1.0)
 
         def store(t, docs):
             nc.sync.dma_start(out[P * t : P * (t + 1), docs], y[t][:, docs])
 
-        for q in range(3):
-            gather(q)
-        round_weights(0)
-        quantise(0)
-        gather(3)
-        round_weights(1)
-        quantise(1)
-        round_weights(2)
-        round_weights(3)
-        for t in range(2):
-            multiply(t, 0)
-            multiply(t, 1)
-        reduce_whole(0, 0)
-        reduce_whole(0, 1)
+        reduce_whole(0)
         quantise(2)
-        multiply(2, 0)
-        multiply(2, 1)
-        reduce_whole(1, 0)
+        reduce_whole(1)
         quantise(3)
-        multiply(3, 0)
-        multiply(3, 1)
-        reduce_whole(1, 1)
+        for t in range(2, TILES):
+            for q in range(4):
+                one_pass(t, q)
+        pairs(1, 0)
+        pairs(1, 1)
+        pairs(2, 0)
+        largest(1, both)
+        pairs(2, 1)
         log_of(0, both)
         store(0, both)
-        relu_low(2, 0)
-        pairs(2, 0)
-        relu_low(2, 1)
-        pairs(2, 1)
-        log_of(1, both)
-        store(1, both)
-        relu_low(3, 0)
         pairs(3, 0)
         largest(2, both)
-        relu_low(3, 1)
         pairs(3, 1)
-        log_of(2, both)
-        store(2, both)
+        for t in (1, 2):
+            log_of(t, both)
+            store(t, both)
         for docs in halves:
             largest(3, docs)
             log_of(3, docs)

@@ -68,7 +68,7 @@ def tile_picked_ysplade_max_p_kernel(tc, x_words, x_scales, w1, bias, offs, out)
         x_sc = keep.tile([P, S], U8, name="x_sc", align_bytes=64)
         nc.vector.memset(x_sc[:].bitcast(I32), 0)
         for q in range(P // QUADRANT):
-            nc.sync.dma_start(x_sc[QUADRANT * q : QUADRANT * q + 4, :].bitcast(I32), picked_sc[TABLE_ROW + 4 * q : TABLE_ROW + 4 * q + 4, :].bitcast(I32))
+            (nc.sync, nc.scalar)[q % 2].dma_start(x_sc[QUADRANT * q : QUADRANT * q + 4, :].bitcast(I32), picked_sc[TABLE_ROW + 4 * q : TABLE_ROW + 4 * q + 4, :].bitcast(I32))
         w_second = placed.tile([P, PACK, P], F32, name="w_second", offset=0, align_bytes=64)
         nc.sync.dma_start(w_second[:], w_rows[:, :, P : 2 * P])
         w_two = placed.tile([P, PACK, 2 * P], F32, name="w_two", offset=2048, align_bytes=64)

@@ -125,7 +125,7 @@ def tile_picked_ysplade_max_p_kernel(tc, x_words, x_scales, w1, bias, offs, out)
         round_weights(2)
         round_weights(3)
 
-        best = [keep.tile([P, 2 * DOCS], F32, name="best%d" % t) for t in range(TILES)]
+        best = {t: keep.tile([P, 2 * DOCS], F32, name="best%d" % t) for t in range(1, TILES)}
         pair = {t: keep.tile([P, 2, 2 * DOCS], F32, name="pair%d" % t) for t in range(1, TILES)}
         low_all = placed.tile([P, 6, 2, DOCS], F32, name="low_all", offset=4096, align_bytes=64)
         y = [keep.tile([P, 2 * DOCS], F32, name="y%d" % t) for t in range(TILES)]
@@ -135,9 +135,8 @@ def tile_picked_ysplade_max_p_kernel(tc, x_words, x_scales, w1, bias, offs, out)
             if h == 0:
                 raw[h] = placed.tile([P, DOCS], F32, name="raw0", offset=1024, align_bytes=64)
             else:
-                raw[h] = keep.tile([P, DOCS], F32, name="raw1", tag="grouped2", align_bytes=64)
+                raw[h] = placed.tile([P, DOCS], F32, name="raw1", offset=2048, align_bytes=64)
             nc.vector.tensor_reduce(raw[h][:], acc[0, h][:].rearrange("p (v d) -> p v d", d=D), mybir.AxisListType.X, ALU.max)
-            nc.gpsimd.tensor_scalar(best[0][:, halves[h]], raw[h][:], LARGEST, b_neg[:], ALU.min, ALU.max)
 
         def pairs(t, h):
             tokens = acc[t, h][:].rearrange("p (v d) -> p d v", d=D)
@@ -157,8 +156,11 @@ def tile_picked_ysplade_max_p_kernel(tc, x_words, x_scales, w1, bias, offs, out)
 
         reduce_whole(0)
         quantise(2)
-        reduce_whole(1)
         quantise(3)
+        reduce_whole(1)
+        best[0] = keep.tile([P, 2 * DOCS], F32, name="best0", tag="grouped3", align_bytes=64)
+        for h in range(2):
+            nc.gpsimd.tensor_scalar(best[0][:, halves[h]], raw[h][:], LARGEST, b_neg[:], ALU.min, ALU.max)
         for t in range(2, TILES):
             for q in range(4):
                 one_pass(t, q)

@@ -77,8 +77,6 @@ def tile_picked_ysplade_max_p_kernel(tc, x_words, x_scales, w1, bias, offs, out)
 
         b_neg = keep.tile([P, 1], F32, name="b_neg")
         nc.scalar.mul(b_neg[:], b_col[:, :1], -1.0)
-        b_one = keep.tile([P, 1], F32, name="b_one")
-        nc.scalar.add(b_one[:], b_col[:, :1], 1.0)
 
         x_codes, rounded, w_codes, w_sc, acc, low, raw = {}, {}, {}, {}, {}, {}, {}
 
@@ -125,7 +123,7 @@ def tile_picked_ysplade_max_p_kernel(tc, x_words, x_scales, w1, bias, offs, out)
         round_weights(2)
         round_weights(3)
 
-        best = {t: keep.tile([P, 2 * DOCS], F32, name="best%d" % t) for t in range(1, TILES)}
+        best = {t: keep.tile([P, 2 * DOCS], F32, name="best%d" % t) for t in range(2, TILES)}
         pair = {t: keep.tile([P, 2, 2 * DOCS], F32, name="pair%d" % t) for t in range(1, TILES)}
         low_all = placed.tile([P, 6, 2, DOCS], F32, name="low_all", offset=4096, align_bytes=64)
         y = [keep.tile([P, 2 * DOCS], F32, name="y%d" % t) for t in range(TILES)]
@@ -149,7 +147,7 @@ def tile_picked_ysplade_max_p_kernel(tc, x_words, x_scales, w1, bias, offs, out)
             nc.vector.tensor_tensor(best[t][:, docs], pair[t][:, 0, docs], pair[t][:, 1, docs], ALU.max)
 
         def log_of(t, docs):
-            nc.scalar.activation(y[t][:, docs], best[t][:, docs], ACT.Ln, bias=b_one[:] if t == 0 else 1.0)
+            nc.scalar.activation(y[t][:, docs], best[t][:, docs], ACT.Ln, bias=1.0)
 
         def store(t, docs):
             nc.sync.dma_start(out[P * t : P * (t + 1), docs], y[t][:, docs])
@@ -158,17 +156,20 @@ def tile_picked_ysplade_max_p_kernel(tc, x_words, x_scales, w1, bias, offs, out)
         quantise(2)
         quantise(3)
         reduce_whole(1)
-        best[0] = keep.tile([P, 2 * DOCS], F32, name="best0", tag="grouped3", align_bytes=64)
+        clamped = keep.tile([P, 2 * DOCS], F32, name="clamped", tag="grouped3", align_bytes=64)
         for h in range(2):
-            nc.gpsimd.tensor_scalar(best[0][:, halves[h]], raw[h][:], LARGEST, b_neg[:], ALU.min, ALU.max)
+            nc.gpsimd.tensor_scalar(clamped[:, halves[h]], raw[h][:], LARGEST, b_neg[:], ALU.min, ALU.max)
+        best[0] = keep.tile([P, 2 * DOCS], F32, name="best0")
+        nc.gpsimd.tensor_scalar(best[0][:], clamped[:], b_col[:, 0:1], 1.0, ALU.add, ALU.mult)
         for t in range(2, TILES):
             for q in range(4):
                 one_pass(t, q)
         pairs(1, 0)
         pairs(1, 1)
         pairs(2, 0)
-        largest(1, both)
         pairs(2, 1)
+        best[1] = placed.tile([P, 2 * DOCS], F32, name="best1", offset=2048, align_bytes=64)
+        largest(1, both)
         log_of(0, both)
         store(0, both)
         pairs(3, 0)

@@ -19,14 +19,20 @@ ALU = mybir.AluOpType
 P = 128
 PACK = 4
 HALF = 512
+QUARTER = HALF // 2
 DOCS = HALF // D
 TILES = N // P
 LIST_GROUP = 16
 QUADRANT = 32
-BLOCK_ROWS = 8
-TABLE_ROW = 112
-LARGEST = 3.4028234663852886e38
-QUARTER = HALF // 2
+SCALE_ROWS = 4
+TABLE_ROW = P - K // 32
+RUN = 4
+
+ALIGN = 64
+SECOND_AT = 0
+RAW_FIRST_AT = SECOND_AT + 4 * QUARTER
+LATE_AT = SECOND_AT + 4 * PACK * P
+LOW_AT = LATE_AT + 4 * PACK * P
 
 
 def tile_picked_ysplade_max_p_kernel(tc, x_words, x_scales, w1, bias, offs, out):
@@ -36,24 +42,24 @@ def tile_picked_ysplade_max_p_kernel(tc, x_words, x_scales, w1, bias, offs, out)
         placed = ctx.enter_context(tc.tile_pool(name="placed", bufs=1))
         psum = ctx.enter_context(tc.psum_pool(name="psum", bufs=1))
 
-        scale_table = placed.tile([P, T], U8, name="scale_table", offset=0, align_bytes=64)
+        scale_table = placed.tile([P, T], U8, name="scale_table", offset=SECOND_AT, align_bytes=ALIGN)
         nc.sync.dma_start(scale_table[TABLE_ROW:, :].bitcast(I32), x_scales[0].bitcast(I32))
         nc.vector.memset(scale_table[:TABLE_ROW, :].bitcast(I32), 0)
         offsets = keep.tile([P, S // LIST_GROUP], U16, name="offsets")
         nc.sync.dma_start(offsets[:], offs)
         b_rows = keep.tile([P, P], F32, name="b_rows")
         nc.scalar.dma_start(b_rows[P - TILES :, :], bias.rearrange("(t p) o -> t (p o)", p=P))
-        word_table = keep.tile([P, T], I32, name="word_table", tag="words", align_bytes=64)
+        word_table = keep.tile([P, T], I32, name="word_table", align_bytes=ALIGN)
         nc.sync.dma_start(word_table[:], x_words[0].rearrange("p n t -> p (n t)").bitcast(I32))
         w_rows = w1.rearrange("(p j) n -> p j n", j=PACK)
-        w_first = keep.tile([P, PACK, P], F32, name="w_first", tag="w_first", align_bytes=64)
+        w_first = keep.tile([P, PACK, P], F32, name="w_first", tag="w_first", align_bytes=ALIGN)
         nc.sync.dma_start(w_first[:], w_rows[:, :, :P])
 
         nc.vector.memset(b_rows[: P - TILES, :], 0.0)
         identity = keep.tile([P, P], F32, name="identity")
         nc.vector.memset(identity[:], 0.0)
         make_identity(nc, identity[:], nomemset=True)
-        b_turned = psum.tile([P, P], F32, name="b_turned", tag="acc3_1")
+        b_turned = psum.tile([P, P], F32, name="b_turned", tag="acc%d_%d" % (TILES - 1, 1))
         nc.tensor.transpose(b_turned[:], b_rows[:], identity[:])
         b_col = keep.tile([P, TILES], F32, name="b_col")
         nc.scalar.copy(b_col[:], b_turned[:, P - TILES :])
@@ -63,40 +69,41 @@ def tile_picked_ysplade_max_p_kernel(tc, x_words, x_scales, w1, bias, offs, out)
         warm = keep.tile([P, 1], F32, name="warm")
         nc.scalar.activation(warm[:], one[:], ACT.Ln)
 
-        picked_sc = keep.tile([P, S], U8, name="picked_sc", align_bytes=64)
+        picked_sc = keep.tile([P, S], U8, name="picked_sc", align_bytes=ALIGN)
         nc.vector.tensor_copy(picked_sc[:], scale_table[:].indirect(offsets[:]))
-        x_sc = keep.tile([P, S], U8, name="x_sc", align_bytes=64)
+        x_sc = keep.tile([P, S], U8, name="x_sc", align_bytes=ALIGN)
         nc.vector.memset(x_sc[:].bitcast(I32), 0)
-        for q in range(P // QUADRANT):
-            (nc.sync, nc.scalar)[q % 2].dma_start(x_sc[QUADRANT * q : QUADRANT * q + 4, :].bitcast(I32), picked_sc[TABLE_ROW + 4 * q : TABLE_ROW + 4 * q + 4, :].bitcast(I32))
-        w_second = placed.tile([P, PACK, P], F32, name="w_second", offset=0, align_bytes=64)
+        for quad in range(P // QUADRANT):
+            source = TABLE_ROW + SCALE_ROWS * quad
+            (nc.sync, nc.scalar)[quad % 2].dma_start(
+                x_sc[QUADRANT * quad : QUADRANT * quad + SCALE_ROWS, :].bitcast(I32),
+                picked_sc[source : source + SCALE_ROWS, :].bitcast(I32),
+            )
+        w_second = placed.tile([P, PACK, P], F32, name="w_second", offset=SECOND_AT, align_bytes=ALIGN)
         nc.sync.dma_start(w_second[:], w_rows[:, :, P : 2 * P])
-        w_two = placed.tile([P, PACK, 2 * P], F32, name="w_two", offset=2048, align_bytes=64)
-        nc.sync.dma_start(w_two[:], w_rows[:, :, 2 * P :])
-        w_raw = [w_first[:], w_second[:], w_two[:, :, :P], w_two[:, :, P:]]
+        w_late = placed.tile([P, PACK, 2 * P], F32, name="w_late", offset=LATE_AT, align_bytes=ALIGN)
+        nc.sync.dma_start(w_late[:], w_rows[:, :, 2 * P :])
+        w_raw = [w_first[:], w_second[:], w_late[:, :, :P], w_late[:, :, P:]]
 
-        b_neg = keep.tile([P, 1], F32, name="b_neg")
-        nc.scalar.mul(b_neg[:], b_col[:, :1], -1.0)
-
-        x_codes, rounded, w_codes, w_sc, acc, low, raw = {}, {}, {}, {}, {}, {}, {}
+        x_codes, rounded, w_codes, w_sc, acc = {}, {}, {}, {}, {}
 
         def gather(q):
             if q == 2:
-                x_codes[q] = keep.tile([P, QUARTER], U32, name="x_codes2", tag="w_first", align_bytes=64)
+                x_codes[q] = keep.tile([P, QUARTER], U32, name="x_codes2", tag="w_first", align_bytes=ALIGN)
             elif q == 3:
-                x_codes[q] = placed.tile([P, QUARTER], U32, name="x_codes3", offset=0, align_bytes=64)
+                x_codes[q] = placed.tile([P, QUARTER], U32, name="x_codes3", offset=SECOND_AT, align_bytes=ALIGN)
             else:
-                x_codes[q] = keep.tile([P, QUARTER], U32, name="x_codes%d" % q, align_bytes=64)
+                x_codes[q] = keep.tile([P, QUARTER], U32, name="x_codes%d" % q, align_bytes=ALIGN)
             columns = slice(q * QUARTER // LIST_GROUP, (q + 1) * QUARTER // LIST_GROUP)
             nc.vector.tensor_copy(x_codes[q][:], word_table[:].bitcast(U32).indirect(offsets[:, columns]))
 
         def round_weights(t):
-            rounded[t] = keep.tile([P, P, PACK], BF16, name="grouped%d" % t, tag="grouped%d" % t, align_bytes=64)
-            nc.scalar.copy(rounded[t][:].rearrange("p (c i) j -> p c j i", i=4), w_raw[t].rearrange("p j (c i) -> p c j i", i=4))
+            rounded[t] = keep.tile([P, P, PACK], BF16, name="rounded%d" % t, tag="rounded%d" % t, align_bytes=ALIGN)
+            nc.scalar.copy(rounded[t][:].rearrange("p (c i) j -> p c j i", i=RUN), w_raw[t].rearrange("p j (c i) -> p c j i", i=RUN))
 
         def quantise(t):
-            w_codes[t] = keep.tile([P, P], U32, name="w_codes%d" % t, align_bytes=64)
-            w_sc[t] = keep.tile([P, P], U8, name="w_sc%d" % t, align_bytes=64)
+            w_codes[t] = keep.tile([P, P], U32, name="w_codes%d" % t, align_bytes=ALIGN)
+            w_sc[t] = keep.tile([P, P], U8, name="w_sc%d" % t, align_bytes=ALIGN)
             nc.vector.quantize_mx(out=w_codes[t][:].bitcast(FP8X4), scales=w_sc[t][:], in_=rounded[t][:].rearrange("p m j -> p (m j)"))
 
         def one_pass(t, q):
@@ -118,23 +125,29 @@ def tile_picked_ysplade_max_p_kernel(tc, x_words, x_scales, w1, bias, offs, out)
             round_weights(t)
             quantise(t)
             gather(2 + t)
-        for t, q in [(0, 0), (0, 1), (0, 2), (1, 0), (1, 1), (0, 3), (1, 2), (1, 3)]:
-            one_pass(t, q)
+        for q in range(3):
+            one_pass(0, q)
+        for q in range(2):
+            one_pass(1, q)
+        one_pass(0, 3)
+        for q in range(2, 4):
+            one_pass(1, q)
         round_weights(2)
         round_weights(3)
 
-        best = {t: keep.tile([P, 2 * DOCS], F32, name="best%d" % t) for t in range(2, TILES)}
+        best = {t: keep.tile([P, 2 * DOCS], F32, name="best%d" % t) for t in range(1, TILES)}
         pair = {t: keep.tile([P, 2, 2 * DOCS], F32, name="pair%d" % t) for t in range(1, TILES)}
-        low_all = placed.tile([P, 6, 2, DOCS], F32, name="low_all", offset=4096, align_bytes=64)
+        low_all = placed.tile([P, 2 * (TILES - 1), 2, DOCS], F32, name="low_all", offset=LOW_AT, align_bytes=ALIGN)
         y = [keep.tile([P, 2 * DOCS], F32, name="y%d" % t) for t in range(TILES)]
         both, halves = slice(0, 2 * DOCS), [slice(0, DOCS), slice(DOCS, 2 * DOCS)]
+        raw = {}
 
         def reduce_whole(h):
-            if h == 0:
-                raw[h] = placed.tile([P, DOCS], F32, name="raw0", offset=1024, align_bytes=64)
-            else:
-                raw[h] = placed.tile([P, DOCS], F32, name="raw1", offset=2048, align_bytes=64)
+            raw[h] = placed.tile([P, DOCS], F32, name="raw%d" % h, offset=(RAW_FIRST_AT, LATE_AT)[h], align_bytes=ALIGN)
             nc.vector.tensor_reduce(raw[h][:], acc[0, h][:].rearrange("p (v d) -> p v d", d=D), mybir.AxisListType.X, ALU.max)
+
+        def relu_whole(h):
+            nc.vector.tensor_scalar(best[0][:, halves[h]], raw[h][:], b_col[:, 0:1], 0.0, ALU.add, ALU.max)
 
         def pairs(t, h):
             tokens = acc[t, h][:].rearrange("p (v d) -> p d v", d=D)
@@ -156,20 +169,17 @@ def tile_picked_ysplade_max_p_kernel(tc, x_words, x_scales, w1, bias, offs, out)
         quantise(2)
         quantise(3)
         reduce_whole(1)
-        clamped = keep.tile([P, 2 * DOCS], F32, name="clamped", tag="grouped3", align_bytes=64)
-        for h in range(2):
-            nc.gpsimd.tensor_scalar(clamped[:, halves[h]], raw[h][:], LARGEST, b_neg[:], ALU.min, ALU.max)
-        best[0] = keep.tile([P, 2 * DOCS], F32, name="best0")
-        nc.gpsimd.tensor_scalar(best[0][:], clamped[:], b_col[:, 0:1], 1.0, ALU.add, ALU.mult)
+        best[0] = keep.tile([P, 2 * DOCS], F32, name="best0", tag="rounded%d" % (TILES - 1), align_bytes=ALIGN)
+        relu_whole(0)
         for t in range(2, TILES):
             for q in range(4):
                 one_pass(t, q)
         pairs(1, 0)
         pairs(1, 1)
         pairs(2, 0)
-        pairs(2, 1)
-        best[1] = placed.tile([P, 2 * DOCS], F32, name="best1", offset=2048, align_bytes=64)
+        relu_whole(1)
         largest(1, both)
+        pairs(2, 1)
         log_of(0, both)
         store(0, both)
         pairs(3, 0)

@@ -137,7 +137,8 @@ def tile_picked_ysplade_max_p_kernel(tc, x_words, x_scales, w1, bias, offs, out)
 
         best = {t: keep.tile([P, 2 * DOCS], F32, name="best%d" % t) for t in range(1, TILES)}
         pair = {t: keep.tile([P, 2, 2 * DOCS], F32, name="pair%d" % t) for t in range(1, TILES)}
-        low_all = placed.tile([P, 2 * (TILES - 1), 2, DOCS], F32, name="low_all", offset=LOW_AT, align_bytes=ALIGN)
+        low_middle = placed.tile([P, 4, 2, DOCS], F32, name="low_middle", offset=LOW_AT, align_bytes=ALIGN)
+        low = {(t, h): low_middle[:, 2 * (t - 1) + h, :, :] for t in (1, 2) for h in range(2)}
         y = [keep.tile([P, 2 * DOCS], F32, name="y%d" % t) for t in range(TILES)]
         both, halves = slice(0, 2 * DOCS), [slice(0, DOCS), slice(DOCS, 2 * DOCS)]
         raw = {}
@@ -152,9 +153,8 @@ def tile_picked_ysplade_max_p_kernel(tc, x_words, x_scales, w1, bias, offs, out)
         def pairs(t, h):
             tokens = acc[t, h][:].rearrange("p (v d) -> p d v", d=D)
             b = b_col[:, t : t + 1]
-            low = low_all[:, 2 * (t - 1) + h, :, :]
-            nc.scalar.activation(low, tokens[:, 0:2, :], ACT.Relu, bias=b)
-            nc.vector.scalar_tensor_tensor(pair[t][:, :, halves[h]], tokens[:, 2:4, :], b, low, ALU.add, ALU.max)
+            nc.scalar.activation(low[t, h], tokens[:, 0:2, :], ACT.Relu, bias=b)
+            nc.vector.scalar_tensor_tensor(pair[t][:, :, halves[h]], tokens[:, 2:4, :], b, low[t, h], ALU.add, ALU.max)
 
         def largest(t, docs):
             nc.vector.tensor_tensor(best[t][:, docs], pair[t][:, 0, docs], pair[t][:, 1, docs], ALU.max)
@@ -175,13 +175,16 @@ def tile_picked_ysplade_max_p_kernel(tc, x_words, x_scales, w1, bias, offs, out)
             for q in range(4):
                 one_pass(t, q)
         pairs(1, 0)
+        relu_whole(1)
         pairs(1, 1)
         pairs(2, 0)
-        relu_whole(1)
         largest(1, both)
         pairs(2, 1)
         log_of(0, both)
         store(0, both)
+        low_last = placed.tile([P, 2, 2, DOCS], F32, name="low_last", offset=LATE_AT, align_bytes=ALIGN)
+        for h in range(2):
+            low[3, h] = low_last[:, h, :, :]
         pairs(3, 0)
         largest(2, both)
         pairs(3, 1)

@@ -32,7 +32,8 @@ ALIGN = 64
 SECOND_AT = 0
 RAW_FIRST_AT = SECOND_AT + 4 * QUARTER
 LATE_AT = SECOND_AT + 4 * PACK * P
-LOW_AT = LATE_AT + 4 * PACK * P
+BEST_AT = LATE_AT + 4 * PACK * P
+LOW_AT = BEST_AT + 4 * 2 * DOCS
 
 
 def tile_picked_ysplade_max_p_kernel(tc, x_words, x_scales, w1, bias, offs, out):
@@ -98,7 +99,7 @@ def tile_picked_ysplade_max_p_kernel(tc, x_words, x_scales, w1, bias, offs, out)
             nc.vector.tensor_copy(x_codes[q][:], word_table[:].bitcast(U32).indirect(offsets[:, columns]))
 
         def round_weights(t):
-            rounded[t] = keep.tile([P, P, PACK], BF16, name="rounded%d" % t, tag="rounded%d" % t, align_bytes=ALIGN)
+            rounded[t] = keep.tile([P, P, PACK], BF16, name="rounded%d" % t, align_bytes=ALIGN)
             nc.scalar.copy(rounded[t][:].rearrange("p (c i) j -> p c j i", i=RUN), w_raw[t].rearrange("p j (c i) -> p c j i", i=RUN))
 
         def quantise(t):
@@ -168,9 +169,9 @@ def tile_picked_ysplade_max_p_kernel(tc, x_words, x_scales, w1, bias, offs, out)
         reduce_whole(0)
         quantise(2)
         quantise(3)
-        reduce_whole(1)
-        best[0] = keep.tile([P, 2 * DOCS], F32, name="best0", tag="rounded%d" % (TILES - 1), align_bytes=ALIGN)
+        best[0] = placed.tile([P, 2 * DOCS], F32, name="best0", offset=BEST_AT, align_bytes=ALIGN)
         relu_whole(0)
+        reduce_whole(1)
         for t in range(2, TILES):
             for q in range(4):
                 one_pass(t, q)

@@ -25,15 +25,14 @@ TILES = N // P
 LIST_GROUP = 16
 QUADRANT = 32
 SCALE_ROWS = 4
-TABLE_ROW = P - K // 32
 RUN = 4
-
 ALIGN = 64
-SECOND_AT = 0
-RAW_FIRST_AT = SECOND_AT + 4 * QUARTER
-LATE_AT = SECOND_AT + 4 * PACK * P
-BEST_AT = LATE_AT + 4 * PACK * P
-LOW_AT = BEST_AT + 4 * 2 * DOCS
+ROW_FIRST, ROW_STEP = 32, 4
+EARLY_WORDS = 1024
+
+RAW_BYTES = 4 * PACK * P
+RAW_AT = {t: RAW_BYTES * (t - 1) for t in (1, 2, 3)}
+TABLE_AT = RAW_AT[2] + RAW_BYTES // 2
 
 
 def tile_picked_ysplade_max_p_kernel(tc, x_words, x_scales, w1, bias, offs, out):
@@ -43,18 +42,29 @@ def tile_picked_ysplade_max_p_kernel(tc, x_words, x_scales, w1, bias, offs, out)
         placed = ctx.enter_context(tc.tile_pool(name="placed", bufs=1))
         psum = ctx.enter_context(tc.psum_pool(name="psum", bufs=1))
 
-        scale_table = placed.tile([P, T], U8, name="scale_table", offset=SECOND_AT, align_bytes=ALIGN)
-        nc.sync.dma_start(scale_table[TABLE_ROW:, :].bitcast(I32), x_scales[0].bitcast(I32))
-        nc.vector.memset(scale_table[:TABLE_ROW, :].bitcast(I32), 0)
+        scale_table = placed.tile([P, T], U8, name="scale_table", offset=TABLE_AT, align_bytes=ALIGN)
+        nc.vector.memset(scale_table[:].bitcast(I32), 0)
+
+        word_table = keep.tile([P, T], I32, name="word_table", align_bytes=256)
+        words = x_words[0].rearrange("p n t -> p (n t)").bitcast(I32)
+        nc.sync.dma_start(word_table[:, :EARLY_WORDS], words[:, :EARLY_WORDS])
         offsets = keep.tile([P, S // LIST_GROUP], U16, name="offsets")
         nc.sync.dma_start(offsets[:], offs)
         b_rows = keep.tile([P, P], F32, name="b_rows")
-        nc.scalar.dma_start(b_rows[P - TILES :, :], bias.rearrange("(t p) o -> t (p o)", p=P))
-        word_table = keep.tile([P, T], I32, name="word_table", align_bytes=ALIGN)
-        nc.sync.dma_start(word_table[:], x_words[0].rearrange("p n t -> p (n t)").bitcast(I32))
+        nc.sync.dma_start(b_rows[P - TILES :, :], bias.rearrange("(t p) o -> t (p o)", p=P))
+        rows = slice(ROW_FIRST, ROW_FIRST + ROW_STEP * (K // 32), ROW_STEP)
+        nc.sync.dma_start(scale_table[rows, :].bitcast(I32), x_scales[0].bitcast(I32))
+        nc.sync.dma_start(word_table[:, EARLY_WORDS:], words[:, EARLY_WORDS:])
         w_rows = w1.rearrange("(p j) n -> p j n", j=PACK)
-        w_first = keep.tile([P, PACK, P], F32, name="w_first", tag="w_first", align_bytes=ALIGN)
-        nc.sync.dma_start(w_first[:], w_rows[:, :, :P])
+        raw = {0: keep.tile([P, PACK, P], F32, name="raw0", tag="raw0", align_bytes=ALIGN)}
+        nc.sync.dma_start(raw[0][:], w_rows[:, :, :P])
+        raw[1] = placed.tile([P, PACK, P], F32, name="raw1", offset=RAW_AT[1], align_bytes=ALIGN)
+        nc.sync.dma_start(raw[1][:], w_rows[:, :, P : 2 * P])
+
+        one = keep.tile([P, 1], F32, name="one")
+        nc.vector.memset(one[:], 1.0)
+        warm = keep.tile([P, 1], F32, name="warm")
+        nc.scalar.activation(warm[:], one[:], ACT.Ln)
 
         nc.vector.memset(b_rows[: P - TILES, :], 0.0)
         identity = keep.tile([P, P], F32, name="identity")
@@ -65,47 +75,42 @@ def tile_picked_ysplade_max_p_kernel(tc, x_words, x_scales, w1, bias, offs, out)
         b_col = keep.tile([P, TILES], F32, name="b_col")
         nc.scalar.copy(b_col[:], b_turned[:, P - TILES :])
 
-        one = keep.tile([P, 1], F32, name="one")
-        nc.vector.memset(one[:], 1.0)
-        warm = keep.tile([P, 1], F32, name="warm")
-        nc.scalar.activation(warm[:], one[:], ACT.Ln)
-
-        picked_sc = keep.tile([P, S], U8, name="picked_sc", align_bytes=ALIGN)
-        nc.vector.tensor_copy(picked_sc[:], scale_table[:].indirect(offsets[:]))
         x_sc = keep.tile([P, S], U8, name="x_sc", align_bytes=ALIGN)
         nc.vector.memset(x_sc[:].bitcast(I32), 0)
+        picked_sc = keep.tile([P, S], U8, name="picked_sc", align_bytes=ALIGN)
+        nc.vector.tensor_copy(picked_sc[:], scale_table[:].indirect(offsets[:]))
         for quad in range(P // QUADRANT):
-            source = TABLE_ROW + SCALE_ROWS * quad
+            source = ROW_FIRST + ROW_STEP * SCALE_ROWS * quad
             (nc.sync, nc.scalar)[quad % 2].dma_start(
                 x_sc[QUADRANT * quad : QUADRANT * quad + SCALE_ROWS, :].bitcast(I32),
-                picked_sc[source : source + SCALE_ROWS, :].bitcast(I32),
+                picked_sc[source : source + ROW_STEP * SCALE_ROWS : ROW_STEP, :].bitcast(I32),
             )
-        w_second = placed.tile([P, PACK, P], F32, name="w_second", offset=SECOND_AT, align_bytes=ALIGN)
-        nc.sync.dma_start(w_second[:], w_rows[:, :, P : 2 * P])
-        w_late = placed.tile([P, PACK, 2 * P], F32, name="w_late", offset=LATE_AT, align_bytes=ALIGN)
-        nc.sync.dma_start(w_late[:], w_rows[:, :, 2 * P :])
-        w_raw = [w_first[:], w_second[:], w_late[:, :, :P], w_late[:, :, P:]]
+        for t in range(2, TILES):
+            raw[t] = placed.tile([P, PACK, P], F32, name="raw%d" % t, offset=RAW_AT[t], align_bytes=ALIGN)
+            nc.sync.dma_start(raw[t][:], w_rows[:, :, P * t : P * (t + 1)])
 
-        x_codes, rounded, w_codes, w_sc, acc = {}, {}, {}, {}, {}
+        x_codes, w_codes, w_sc, acc = {}, {}, {}, {}
+        rounded_all = keep.tile([P, N, PACK], BF16, name="rounded_all", align_bytes=ALIGN)
+        rounded = [rounded_all[:, P * t : P * (t + 1), :] for t in range(TILES)]
 
         def gather(q):
             if q == 2:
-                x_codes[q] = keep.tile([P, QUARTER], U32, name="x_codes2", tag="w_first", align_bytes=ALIGN)
-            elif q == 3:
-                x_codes[q] = placed.tile([P, QUARTER], U32, name="x_codes3", offset=SECOND_AT, align_bytes=ALIGN)
+                x_codes[q] = keep.tile([P, QUARTER], U32, name="x_codes2", tag="raw0", align_bytes=ALIGN)
             else:
-                x_codes[q] = keep.tile([P, QUARTER], U32, name="x_codes%d" % q, align_bytes=ALIGN)
+                x_codes[q] = placed.tile([P, QUARTER], U32, name="x_codes3", offset=RAW_AT[1], align_bytes=ALIGN)
             columns = slice(q * QUARTER // LIST_GROUP, (q + 1) * QUARTER // LIST_GROUP)
             nc.vector.tensor_copy(x_codes[q][:], word_table[:].bitcast(U32).indirect(offsets[:, columns]))
 
         def round_weights(t):
-            rounded[t] = keep.tile([P, P, PACK], BF16, name="rounded%d" % t, align_bytes=ALIGN)
-            nc.scalar.copy(rounded[t][:].rearrange("p (c i) j -> p c j i", i=RUN), w_raw[t].rearrange("p j (c i) -> p c j i", i=RUN))
+            nc.scalar.copy(rounded[t].rearrange("p (c i) j -> p c j i", i=RUN), raw[t][:].rearrange("p j (c i) -> p c j i", i=RUN))
 
-        def quantise(t):
-            w_codes[t] = keep.tile([P, P], U32, name="w_codes%d" % t, align_bytes=ALIGN)
-            w_sc[t] = keep.tile([P, P], U8, name="w_sc%d" % t, align_bytes=ALIGN)
-            nc.vector.quantize_mx(out=w_codes[t][:].bitcast(FP8X4), scales=w_sc[t][:], in_=rounded[t][:].rearrange("p m j -> p (m j)"))
+        def quantise(tiles):
+            codes = keep.tile([P, P * len(tiles)], U32, name="w_codes%d" % tiles[0], align_bytes=ALIGN)
+            scales = keep.tile([P, P * len(tiles)], U8, name="w_sc%d" % tiles[0], align_bytes=ALIGN)
+            columns = rounded_all[:, P * tiles[0] : P * (tiles[-1] + 1), :]
+            nc.vector.quantize_mx(out=codes[:].bitcast(FP8X4), scales=scales[:], in_=columns.rearrange("p m j -> p (m j)"))
+            for i, t in enumerate(tiles):
+                w_codes[t], w_sc[t] = codes[:, P * i : P * (i + 1)], scales[:, P * i : P * (i + 1)]
 
         def one_pass(t, q):
             if q % 2 == 0:
@@ -120,11 +125,12 @@ def tile_picked_ysplade_max_p_kernel(tc, x_words, x_scales, w1, bias, offs, out)
                 stop=True,
             )
 
-        gather(0)
-        gather(1)
+        x_first = keep.tile([P, HALF], U32, name="x_first", align_bytes=ALIGN)
+        nc.vector.tensor_copy(x_first[:], word_table[:].bitcast(U32).indirect(offsets[:, : HALF // LIST_GROUP]))
+        x_codes[0], x_codes[1] = x_first[:, :QUARTER], x_first[:, QUARTER:]
         for t in range(2):
             round_weights(t)
-            quantise(t)
+            quantise([t])
             gather(2 + t)
         for q in range(3):
             one_pass(0, q)
@@ -137,62 +143,47 @@ def tile_picked_ysplade_max_p_kernel(tc, x_words, x_scales, w1, bias, offs, out)
         round_weights(3)
 
         best = {t: keep.tile([P, 2 * DOCS], F32, name="best%d" % t) for t in range(1, TILES)}
-        pair = {t: keep.tile([P, 2, 2 * DOCS], F32, name="pair%d" % t) for t in range(1, TILES)}
-        low_middle = placed.tile([P, 4, 2, DOCS], F32, name="low_middle", offset=LOW_AT, align_bytes=ALIGN)
-        low = {(t, h): low_middle[:, 2 * (t - 1) + h, :, :] for t in (1, 2) for h in range(2)}
+        pair = {t: keep.tile([P, 2, 2 * DOCS], F32, name="pair%d" % t) for t in range(TILES)}
         y = [keep.tile([P, 2 * DOCS], F32, name="y%d" % t) for t in range(TILES)]
         both, halves = slice(0, 2 * DOCS), [slice(0, DOCS), slice(DOCS, 2 * DOCS)]
-        raw = {}
-
-        def reduce_whole(h):
-            raw[h] = placed.tile([P, DOCS], F32, name="raw%d" % h, offset=(RAW_FIRST_AT, LATE_AT)[h], align_bytes=ALIGN)
-            nc.vector.tensor_reduce(raw[h][:], acc[0, h][:].rearrange("p (v d) -> p v d", d=D), mybir.AxisListType.X, ALU.max)
-
-        def relu_whole(h):
-            nc.vector.tensor_scalar(best[0][:, halves[h]], raw[h][:], b_col[:, 0:1], 0.0, ALU.add, ALU.max)
+        low_all = placed.tile([P, 2 * TILES, 2, DOCS], F32, name="low_all", offset=RAW_AT[3] + RAW_BYTES // 2, align_bytes=ALIGN)
+        best[0] = placed.tile([P, 2 * DOCS], F32, name="best0", offset=RAW_AT[3], align_bytes=ALIGN)
+        whole = placed.tile([P, DOCS], F32, name="whole", offset=RAW_AT[1] + RAW_BYTES // 2, align_bytes=ALIGN)
 
         def pairs(t, h):
             tokens = acc[t, h][:].rearrange("p (v d) -> p d v", d=D)
             b = b_col[:, t : t + 1]
-            nc.scalar.activation(low[t, h], tokens[:, 0:2, :], ACT.Relu, bias=b)
-            nc.vector.scalar_tensor_tensor(pair[t][:, :, halves[h]], tokens[:, 2:4, :], b, low[t, h], ALU.add, ALU.max)
+            low = low_all[:, 2 * t + h, :, :]
+            nc.scalar.activation(low, tokens[:, 0:2, :], ACT.Relu, bias=b)
+            nc.vector.scalar_tensor_tensor(pair[t][:, :, halves[h]], tokens[:, 2:4, :], b, low, ALU.add, ALU.max)
 
         def largest(t, docs):
             nc.vector.tensor_tensor(best[t][:, docs], pair[t][:, 0, docs], pair[t][:, 1, docs], ALU.max)
 
-        def log_of(t, docs):
+        def finish(t, docs):
             nc.scalar.activation(y[t][:, docs], best[t][:, docs], ACT.Ln, bias=1.0)
-
-        def store(t, docs):
             nc.sync.dma_start(out[P * t : P * (t + 1), docs], y[t][:, docs])
 
-        reduce_whole(0)
-        quantise(2)
-        quantise(3)
-        best[0] = placed.tile([P, 2 * DOCS], F32, name="best0", offset=BEST_AT, align_bytes=ALIGN)
-        relu_whole(0)
-        reduce_whole(1)
+        nc.vector.tensor_reduce(whole[:], acc[0, 0][:].rearrange("p (v d) -> p v d", d=D), mybir.AxisListType.X, ALU.max)
+        quantise([2])
+        quantise([3])
+        nc.vector.tensor_scalar(best[0][:, halves[0]], whole[:], b_col[:, 0:1], 0.0, ALU.add, ALU.max)
         for t in range(2, TILES):
             for q in range(4):
                 one_pass(t, q)
         pairs(1, 0)
-        relu_whole(1)
+        pairs(0, 1)
         pairs(1, 1)
+        largest(0, halves[1])
         pairs(2, 0)
         largest(1, both)
+        finish(0, both)
         pairs(2, 1)
-        log_of(0, both)
-        store(0, both)
-        low_last = placed.tile([P, 2, 2, DOCS], F32, name="low_last", offset=LATE_AT, align_bytes=ALIGN)
-        for h in range(2):
-            low[3, h] = low_last[:, h, :, :]
+        largest(2, halves[0])
         pairs(3, 0)
-        largest(2, both)
         pairs(3, 1)
-        for t in (1, 2):
-            log_of(t, both)
-            store(t, both)
-        for docs in halves:
-            largest(3, docs)
-            log_of(3, docs)
-            store(3, docs)
+        finish(1, both)
+        finish(2, halves[0])
+        for t, h in ((2, 1), (3, 0), (3, 1)):
+            largest(t, halves[h])
+            finish(t, halves[h])

@@ -25,14 +25,17 @@ TILES = N // P
 LIST_GROUP = 16
 QUADRANT = 32
 SCALE_ROWS = 4
+TABLE_ROW = P - K // 32
 RUN = 4
 ALIGN = 64
-ROW_FIRST, ROW_STEP = 32, 4
-EARLY_WORDS = 1024
+MIDDLE = P
+LAST = N - P - MIDDLE
 
-RAW_BYTES = 4 * PACK * P
-RAW_AT = {t: RAW_BYTES * (t - 1) for t in (1, 2, 3)}
-TABLE_AT = RAW_AT[2] + RAW_BYTES // 2
+FIRST_AT = 0
+MIDDLE_AT = FIRST_AT + 4 * PACK * P
+LAST_AT = MIDDLE_AT + 4 * PACK * MIDDLE
+TABLE_AT = LAST_AT - T // 4
+LOW_AT = LAST_AT + 4 * PACK * LAST - ALIGN
 
 
 def tile_picked_ysplade_max_p_kernel(tc, x_words, x_scales, w1, bias, offs, out):
@@ -43,28 +46,17 @@ def tile_picked_ysplade_max_p_kernel(tc, x_words, x_scales, w1, bias, offs, out)
         psum = ctx.enter_context(tc.psum_pool(name="psum", bufs=1))
 
         scale_table = placed.tile([P, T], U8, name="scale_table", offset=TABLE_AT, align_bytes=ALIGN)
-        nc.vector.memset(scale_table[:].bitcast(I32), 0)
-
-        word_table = keep.tile([P, T], I32, name="word_table", align_bytes=256)
-        words = x_words[0].rearrange("p n t -> p (n t)").bitcast(I32)
-        nc.sync.dma_start(word_table[:, :EARLY_WORDS], words[:, :EARLY_WORDS])
+        nc.sync.dma_start(scale_table[TABLE_ROW:, :].bitcast(I32), x_scales[0].bitcast(I32))
+        nc.vector.memset(scale_table[:TABLE_ROW, :].bitcast(I32), 0)
         offsets = keep.tile([P, S // LIST_GROUP], U16, name="offsets")
         nc.sync.dma_start(offsets[:], offs)
         b_rows = keep.tile([P, P], F32, name="b_rows")
-        nc.sync.dma_start(b_rows[P - TILES :, :], bias.rearrange("(t p) o -> t (p o)", p=P))
-        rows = slice(ROW_FIRST, ROW_FIRST + ROW_STEP * (K // 32), ROW_STEP)
-        nc.sync.dma_start(scale_table[rows, :].bitcast(I32), x_scales[0].bitcast(I32))
-        nc.sync.dma_start(word_table[:, EARLY_WORDS:], words[:, EARLY_WORDS:])
+        nc.scalar.dma_start(b_rows[P - TILES :, :], bias.rearrange("(t p) o -> t (p o)", p=P))
+        word_table = keep.tile([P, T], I32, name="word_table", align_bytes=ALIGN)
+        nc.sync.dma_start(word_table[:], x_words[0].rearrange("p n t -> p (n t)").bitcast(I32))
         w_rows = w1.rearrange("(p j) n -> p j n", j=PACK)
-        raw = {0: keep.tile([P, PACK, P], F32, name="raw0", tag="raw0", align_bytes=ALIGN)}
-        nc.sync.dma_start(raw[0][:], w_rows[:, :, :P])
-        raw[1] = placed.tile([P, PACK, P], F32, name="raw1", offset=RAW_AT[1], align_bytes=ALIGN)
-        nc.sync.dma_start(raw[1][:], w_rows[:, :, P : 2 * P])
-
-        one = keep.tile([P, 1], F32, name="one")
-        nc.vector.memset(one[:], 1.0)
-        warm = keep.tile([P, 1], F32, name="warm")
-        nc.scalar.activation(warm[:], one[:], ACT.Ln)
+        w_first = placed.tile([P, PACK, P], F32, name="w_first", offset=FIRST_AT, align_bytes=ALIGN)
+        nc.sync.dma_start(w_first[:], w_rows[:, :, :P])
 
         nc.vector.memset(b_rows[: P - TILES, :], 0.0)
         identity = keep.tile([P, P], F32, name="identity")
@@ -75,114 +67,131 @@ def tile_picked_ysplade_max_p_kernel(tc, x_words, x_scales, w1, bias, offs, out)
         b_col = keep.tile([P, TILES], F32, name="b_col")
         nc.scalar.copy(b_col[:], b_turned[:, P - TILES :])
 
-        x_sc = keep.tile([P, S], U8, name="x_sc", align_bytes=ALIGN)
-        nc.vector.memset(x_sc[:].bitcast(I32), 0)
+        one = keep.tile([P, 1], F32, name="one")
+        nc.vector.memset(one[:], 1.0)
+        warm = keep.tile([P, 1], F32, name="warm")
+        nc.scalar.activation(warm[:], one[:], ACT.Ln)
+
         picked_sc = keep.tile([P, S], U8, name="picked_sc", align_bytes=ALIGN)
         nc.vector.tensor_copy(picked_sc[:], scale_table[:].indirect(offsets[:]))
+        x_sc = keep.tile([P, S], U8, name="x_sc", align_bytes=ALIGN)
+        nc.vector.memset(x_sc[:].bitcast(I32), 0)
         for quad in range(P // QUADRANT):
-            source = ROW_FIRST + ROW_STEP * SCALE_ROWS * quad
+            source = TABLE_ROW + SCALE_ROWS * quad
             (nc.sync, nc.scalar)[quad % 2].dma_start(
                 x_sc[QUADRANT * quad : QUADRANT * quad + SCALE_ROWS, :].bitcast(I32),
-                picked_sc[source : source + ROW_STEP * SCALE_ROWS : ROW_STEP, :].bitcast(I32),
+                picked_sc[source : source + SCALE_ROWS, :].bitcast(I32),
             )
-        for t in range(2, TILES):
-            raw[t] = placed.tile([P, PACK, P], F32, name="raw%d" % t, offset=RAW_AT[t], align_bytes=ALIGN)
-            nc.sync.dma_start(raw[t][:], w_rows[:, :, P * t : P * (t + 1)])
+        w_middle = placed.tile([P, PACK, MIDDLE], F32, name="w_middle", offset=MIDDLE_AT, align_bytes=ALIGN)
+        nc.sync.dma_start(w_middle[:], w_rows[:, :, P : P + MIDDLE])
+        w_last = placed.tile([P, PACK, LAST], F32, name="w_last", offset=LAST_AT, align_bytes=ALIGN)
+        nc.sync.dma_start(w_last[:], w_rows[:, :, P + MIDDLE :])
 
         x_codes, w_codes, w_sc, acc = {}, {}, {}, {}
-        rounded_all = keep.tile([P, N, PACK], BF16, name="rounded_all", align_bytes=ALIGN)
-        rounded = [rounded_all[:, P * t : P * (t + 1), :] for t in range(TILES)]
+        rounded = keep.tile([P, N, PACK], BF16, name="rounded", align_bytes=ALIGN)
 
-        def gather(q):
-            if q == 2:
-                x_codes[q] = keep.tile([P, QUARTER], U32, name="x_codes2", tag="raw0", align_bytes=ALIGN)
-            else:
-                x_codes[q] = placed.tile([P, QUARTER], U32, name="x_codes3", offset=RAW_AT[1], align_bytes=ALIGN)
-            columns = slice(q * QUARTER // LIST_GROUP, (q + 1) * QUARTER // LIST_GROUP)
-            nc.vector.tensor_copy(x_codes[q][:], word_table[:].bitcast(U32).indirect(offsets[:, columns]))
+        def gather(into, first, entries):
+            columns = slice(first // LIST_GROUP, (first + entries) // LIST_GROUP)
+            nc.vector.tensor_copy(into[:], word_table[:].bitcast(U32).indirect(offsets[:, columns]))
+            for q in range(entries // QUARTER):
+                x_codes[first // QUARTER + q] = into[:, QUARTER * q : QUARTER * (q + 1)]
 
-        def round_weights(t):
-            nc.scalar.copy(rounded[t].rearrange("p (c i) j -> p c j i", i=RUN), raw[t][:].rearrange("p j (c i) -> p c j i", i=RUN))
+        def round_weights(raw, first):
+            into = rounded[:, first : first + raw.shape[2], :]
+            nc.scalar.copy(into.rearrange("p (c i) j -> p c j i", i=RUN), raw.rearrange("p j (c i) -> p c j i", i=RUN))
 
         def quantise(tiles):
             codes = keep.tile([P, P * len(tiles)], U32, name="w_codes%d" % tiles[0], align_bytes=ALIGN)
             scales = keep.tile([P, P * len(tiles)], U8, name="w_sc%d" % tiles[0], align_bytes=ALIGN)
-            columns = rounded_all[:, P * tiles[0] : P * (tiles[-1] + 1), :]
+            columns = rounded[:, P * tiles[0] : P * (tiles[-1] + 1), :]
             nc.vector.quantize_mx(out=codes[:].bitcast(FP8X4), scales=scales[:], in_=columns.rearrange("p m j -> p (m j)"))
             for i, t in enumerate(tiles):
                 w_codes[t], w_sc[t] = codes[:, P * i : P * (i + 1)], scales[:, P * i : P * (i + 1)]
 
-        def one_pass(t, q):
-            if q % 2 == 0:
-                acc[t, q // 2] = psum.tile([P, HALF], F32, name="acc%d_%d" % (t, q // 2), tag="acc%d_%d" % (t, q // 2))
-            nc.tensor.matmul_mx(
-                out=acc[t, q // 2][:, QUARTER * (q % 2) : QUARTER * (q % 2 + 1)],
-                lhsT=w_codes[t][:].bitcast(FP8X4),
-                lhsT_scale=w_sc[t][:],
-                rhs=x_codes[q][:].bitcast(FP8X4),
-                rhs_scale=x_sc[:, QUARTER * q : QUARTER * (q + 1)],
-                start=True,
-                stop=True,
-            )
+        def products(t, quarters):
+            for q in quarters:
+                if q % 2 == 0:
+                    acc[t, q // 2] = psum.tile([P, HALF], F32, name="acc%d_%d" % (t, q // 2), tag="acc%d_%d" % (t, q // 2))
+                nc.tensor.matmul_mx(
+                    out=acc[t, q // 2][:, QUARTER * (q % 2) : QUARTER * (q % 2 + 1)],
+                    lhsT=w_codes[t].bitcast(FP8X4),
+                    lhsT_scale=w_sc[t],
+                    rhs=x_codes[q].bitcast(FP8X4),
+                    rhs_scale=x_sc[:, QUARTER * q : QUARTER * (q + 1)],
+                    start=True,
+                    stop=True,
+                )
 
         x_first = keep.tile([P, HALF], U32, name="x_first", align_bytes=ALIGN)
-        nc.vector.tensor_copy(x_first[:], word_table[:].bitcast(U32).indirect(offsets[:, : HALF // LIST_GROUP]))
-        x_codes[0], x_codes[1] = x_first[:, :QUARTER], x_first[:, QUARTER:]
-        for t in range(2):
-            round_weights(t)
-            quantise([t])
-            gather(2 + t)
-        for q in range(3):
-            one_pass(0, q)
-        for q in range(2):
-            one_pass(1, q)
-        one_pass(0, 3)
-        for q in range(2, 4):
-            one_pass(1, q)
-        round_weights(2)
-        round_weights(3)
+        gather(x_first, 0, HALF)
+        round_weights(w_first[:], 0)
+        quantise([0])
+        x_third = placed.tile([P, QUARTER], U32, name="x_third", offset=FIRST_AT, align_bytes=ALIGN)
+        gather(x_third, HALF, QUARTER)
+        round_weights(w_middle[:, :, :P], P)
+        quantise([1])
+        x_fourth = placed.tile([P, QUARTER], U32, name="x_fourth", offset=MIDDLE_AT, align_bytes=ALIGN)
+        gather(x_fourth, HALF + QUARTER, QUARTER)
+        round_weights(w_last[:, :, :P], 2 * P)
+        round_weights(w_last[:, :, P:], 3 * P)
+        products(0, range(3))
+        products(1, range(2))
+        products(0, [3])
+        products(1, [2, 3])
 
         best = {t: keep.tile([P, 2 * DOCS], F32, name="best%d" % t) for t in range(1, TILES)}
-        pair = {t: keep.tile([P, 2, 2 * DOCS], F32, name="pair%d" % t) for t in range(TILES)}
-        y = [keep.tile([P, 2 * DOCS], F32, name="y%d" % t) for t in range(TILES)]
+        pair = {t: keep.tile([P, 2, 2 * DOCS], F32, name="pair%d" % t) for t in range(1, TILES)}
+        y_all = keep.tile([P, TILES, 2 * DOCS], F32, name="y_all")
+        y = [y_all[:, t, :] for t in range(TILES)]
         both, halves = slice(0, 2 * DOCS), [slice(0, DOCS), slice(DOCS, 2 * DOCS)]
-        low_all = placed.tile([P, 2 * TILES, 2, DOCS], F32, name="low_all", offset=RAW_AT[3] + RAW_BYTES // 2, align_bytes=ALIGN)
-        best[0] = placed.tile([P, 2 * DOCS], F32, name="best0", offset=RAW_AT[3], align_bytes=ALIGN)
-        whole = placed.tile([P, DOCS], F32, name="whole", offset=RAW_AT[1] + RAW_BYTES // 2, align_bytes=ALIGN)
+        late = placed.tile([P, 7, 2, DOCS], F32, name="late", offset=LOW_AT, align_bytes=ALIGN)
+        low = {(t, h): late[:, 2 * (t - 1) + h, :, :] for t in range(1, TILES) for h in range(2)}
+        best[0] = late[:, 6, :, :].rearrange("p h v -> p (h v)")
+        whole = {}
+
+        def reduce_whole(h):
+            whole[h] = placed.tile([P, DOCS], F32, name="whole%d" % h, offset=LAST_AT - 4 * DOCS * (1 - h), align_bytes=ALIGN)
+            nc.vector.tensor_reduce(whole[h][:], acc[0, h][:].rearrange("p (v d) -> p v d", d=D), mybir.AxisListType.X, ALU.max)
+
+        def relu_whole(h):
+            nc.vector.tensor_scalar(best[0][:, halves[h]], whole[h][:], b_col[:, 0:1], 0.0, ALU.add, ALU.max)
 
         def pairs(t, h):
             tokens = acc[t, h][:].rearrange("p (v d) -> p d v", d=D)
             b = b_col[:, t : t + 1]
-            low = low_all[:, 2 * t + h, :, :]
-            nc.scalar.activation(low, tokens[:, 0:2, :], ACT.Relu, bias=b)
-            nc.vector.scalar_tensor_tensor(pair[t][:, :, halves[h]], tokens[:, 2:4, :], b, low, ALU.add, ALU.max)
+            nc.scalar.activation(low[t, h], tokens[:, 0:2, :], ACT.Relu, bias=b)
+            nc.vector.scalar_tensor_tensor(pair[t][:, :, halves[h]], tokens[:, 2:4, :], b, low[t, h], ALU.add, ALU.max)
 
         def largest(t, docs):
             nc.vector.tensor_tensor(best[t][:, docs], pair[t][:, 0, docs], pair[t][:, 1, docs], ALU.max)
 
-        def finish(t, docs):
+        def log_of(t, docs):
             nc.scalar.activation(y[t][:, docs], best[t][:, docs], ACT.Ln, bias=1.0)
+
+        def finish(t, docs):
+            log_of(t, docs)
             nc.sync.dma_start(out[P * t : P * (t + 1), docs], y[t][:, docs])
 
-        nc.vector.tensor_reduce(whole[:], acc[0, 0][:].rearrange("p (v d) -> p v d", d=D), mybir.AxisListType.X, ALU.max)
+        reduce_whole(0)
         quantise([2])
         quantise([3])
-        nc.vector.tensor_scalar(best[0][:, halves[0]], whole[:], b_col[:, 0:1], 0.0, ALU.add, ALU.max)
-        for t in range(2, TILES):
-            for q in range(4):
-                one_pass(t, q)
+        reduce_whole(1)
+        products(2, range(4))
+        products(3, range(4))
         pairs(1, 0)
-        pairs(0, 1)
+        relu_whole(0)
         pairs(1, 1)
-        largest(0, halves[1])
+        relu_whole(1)
+        largest(1, halves[0])
         pairs(2, 0)
-        largest(1, both)
-        finish(0, both)
+        largest(1, halves[1])
         pairs(2, 1)
         largest(2, halves[0])
         pairs(3, 0)
         pairs(3, 1)
-        finish(1, both)
+        log_of(0, both)
+        log_of(1, both)
+        nc.sync.dma_start(out[: 2 * P, :].rearrange("(t p) v -> p t v", p=P), y_all[:, :2, :])
         finish(2, halves[0])
         for t, h in ((2, 1), (3, 0), (3, 1)):
             largest(t, halves[h])

@@ -27,7 +27,7 @@ QUADRANT = 32
 SCALE_ROWS = 4
 TABLE_ROW = P - K // 32
 RUN = 4
-ALIGN = 64
+ALIGN = 256
 MIDDLE = P
 LAST = N - P - MIDDLE
 
@@ -84,8 +84,10 @@ def tile_picked_ysplade_max_p_kernel(tc, x_words, x_scales, w1, bias, offs, out)
             )
         w_middle = placed.tile([P, PACK, MIDDLE], F32, name="w_middle", offset=MIDDLE_AT, align_bytes=ALIGN)
         nc.sync.dma_start(w_middle[:], w_rows[:, :, P : P + MIDDLE])
-        w_last = placed.tile([P, PACK, LAST], F32, name="w_last", offset=LAST_AT, align_bytes=ALIGN)
-        nc.sync.dma_start(w_last[:], w_rows[:, :, P + MIDDLE :])
+        w_last = {}
+        for t in (2, 3):
+            w_last[t] = placed.tile([P, PACK, P], F32, name="w_last%d" % t, offset=LAST_AT + 4 * PACK * P * (t - 2), align_bytes=ALIGN)
+            nc.sync.dma_start(w_last[t][:], w_rows[:, :, P * t : P * (t + 1)])
 
         x_codes, w_codes, w_sc, acc = {}, {}, {}, {}
         rounded = keep.tile([P, N, PACK], BF16, name="rounded", align_bytes=ALIGN)
@@ -132,29 +134,27 @@ def tile_picked_ysplade_max_p_kernel(tc, x_words, x_scales, w1, bias, offs, out)
         quantise([1])
         x_fourth = placed.tile([P, QUARTER], U32, name="x_fourth", offset=MIDDLE_AT, align_bytes=ALIGN)
         gather(x_fourth, HALF + QUARTER, QUARTER)
-        round_weights(w_last[:, :, :P], 2 * P)
-        round_weights(w_last[:, :, P:], 3 * P)
+        round_weights(w_last[2][:], 2 * P)
+        round_weights(w_last[3][:], 3 * P)
         products(0, range(3))
         products(1, range(2))
         products(0, [3])
         products(1, [2, 3])
 
         best = {t: keep.tile([P, 2 * DOCS], F32, name="best%d" % t) for t in range(1, TILES)}
-        pair = {t: keep.tile([P, 2, 2 * DOCS], F32, name="pair%d" % t) for t in range(1, TILES)}
-        y_all = keep.tile([P, TILES, 2 * DOCS], F32, name="y_all")
+        pair = {t: keep.tile([P, 2, 2 * DOCS], F32, name="pair%d" % t) for t in range(TILES)}
+        y_all = keep.tile([P, TILES, 2 * DOCS], F32, name="y_all", align_bytes=ALIGN)
         y = [y_all[:, t, :] for t in range(TILES)]
         both, halves = slice(0, 2 * DOCS), [slice(0, DOCS), slice(DOCS, 2 * DOCS)]
         late = placed.tile([P, 7, 2, DOCS], F32, name="late", offset=LOW_AT, align_bytes=ALIGN)
-        low = {(t, h): late[:, 2 * (t - 1) + h, :, :] for t in range(1, TILES) for h in range(2)}
+        paired = [(0, 1), (1, 1)] + [(t, h) for t in range(2, TILES) for h in range(2)]
+        low = {bank: late[:, i, :, :] for i, bank in enumerate(paired)}
         best[0] = late[:, 6, :, :].rearrange("p h v -> p (h v)")
         whole = {}
 
-        def reduce_whole(h):
-            whole[h] = placed.tile([P, DOCS], F32, name="whole%d" % h, offset=LAST_AT - 4 * DOCS * (1 - h), align_bytes=ALIGN)
-            nc.vector.tensor_reduce(whole[h][:], acc[0, h][:].rearrange("p (v d) -> p v d", d=D), mybir.AxisListType.X, ALU.max)
-
-        def relu_whole(h):
-            nc.vector.tensor_scalar(best[0][:, halves[h]], whole[h][:], b_col[:, 0:1], 0.0, ALU.add, ALU.max)
+        def reduce_whole(t):
+            whole[t] = placed.tile([P, DOCS], F32, name="whole%d" % t, offset=LAST_AT - 4 * DOCS * (1 - t), align_bytes=ALIGN)
+            nc.vector.tensor_reduce(whole[t][:], acc[t, 0][:].rearrange("p (v d) -> p v d", d=D), mybir.AxisListType.X, ALU.max)
 
         def pairs(t, h):
             tokens = acc[t, h][:].rearrange("p (v d) -> p d v", d=D)
@@ -174,15 +174,15 @@ def tile_picked_ysplade_max_p_kernel(tc, x_words, x_scales, w1, bias, offs, out)
 
         reduce_whole(0)
         quantise([2])
-        quantise([3])
         reduce_whole(1)
+        quantise([3])
         products(2, range(4))
         products(3, range(4))
-        pairs(1, 0)
-        relu_whole(0)
+        nc.scalar.activation(best[0][:, halves[0]], whole[0][:], ACT.Relu, bias=b_col[:, 0:1])
+        pairs(0, 1)
+        nc.vector.tensor_scalar(best[1][:, halves[0]], whole[1][:], b_col[:, 1:2], 0.0, ALU.add, ALU.max)
         pairs(1, 1)
-        relu_whole(1)
-        largest(1, halves[0])
+        largest(0, halves[1])
         pairs(2, 0)
         largest(1, halves[1])
         pairs(2, 1)
@@ -192,7 +192,10 @@ def tile_picked_ysplade_max_p_kernel(tc, x_words, x_scales, w1, bias, offs, out)
         log_of(0, both)
         log_of(1, both)
         nc.sync.dma_start(out[: 2 * P, :].rearrange("(t p) v -> p t v", p=P), y_all[:, :2, :])
-        finish(2, halves[0])
-        for t, h in ((2, 1), (3, 0), (3, 1)):
-            largest(t, halves[h])
-            finish(t, halves[h])
+        log_of(2, halves[0])
+        largest(2, halves[1])
+        log_of(2, halves[1])
+        nc.sync.dma_start(out[2 * P : 3 * P, :], y[2])
+        for h in range(2):
+            largest(3, halves[h])
+            finish(3, halves[h])

@@ -34,7 +34,7 @@ LAST = N - P - MIDDLE
 FIRST_AT = 0
 MIDDLE_AT = FIRST_AT + 4 * PACK * P
 LAST_AT = MIDDLE_AT + 4 * PACK * MIDDLE
-TABLE_AT = LAST_AT - T // 4
+TABLE_AT = LAST_AT
 LOW_AT = LAST_AT + 4 * PACK * LAST - ALIGN
 
 
@@ -57,6 +57,8 @@ def tile_picked_ysplade_max_p_kernel(tc, x_words, x_scales, w1, bias, offs, out)
         w_rows = w1.rearrange("(p j) n -> p j n", j=PACK)
         w_first = placed.tile([P, PACK, P], F32, name="w_first", offset=FIRST_AT, align_bytes=ALIGN)
         nc.sync.dma_start(w_first[:], w_rows[:, :, :P])
+        w_middle = placed.tile([P, PACK, MIDDLE], F32, name="w_middle", offset=MIDDLE_AT, align_bytes=ALIGN)
+        nc.sync.dma_start(w_middle[:], w_rows[:, :, P : P + MIDDLE])
 
         nc.vector.memset(b_rows[: P - TILES, :], 0.0)
         identity = keep.tile([P, P], F32, name="identity")
@@ -82,8 +84,6 @@ def tile_picked_ysplade_max_p_kernel(tc, x_words, x_scales, w1, bias, offs, out)
                 x_sc[QUADRANT * quad : QUADRANT * quad + SCALE_ROWS, :].bitcast(I32),
                 picked_sc[source : source + SCALE_ROWS, :].bitcast(I32),
             )
-        w_middle = placed.tile([P, PACK, MIDDLE], F32, name="w_middle", offset=MIDDLE_AT, align_bytes=ALIGN)
-        nc.sync.dma_start(w_middle[:], w_rows[:, :, P : P + MIDDLE])
         w_last = {}
         for t in (2, 3):
             w_last[t] = placed.tile([P, PACK, P], F32, name="w_last%d" % t, offset=LAST_AT + 4 * PACK * P * (t - 2), align_bytes=ALIGN)

@@ -141,20 +141,20 @@ def tile_picked_ysplade_max_p_kernel(tc, x_words, x_scales, w1, bias, offs, out)
         products(0, [3])
         products(1, [2, 3])
 
-        best = {t: keep.tile([P, 2 * DOCS], F32, name="best%d" % t) for t in range(1, TILES)}
-        pair = {t: keep.tile([P, 2, 2 * DOCS], F32, name="pair%d" % t) for t in range(TILES)}
+        best = {t: keep.tile([P, 2 * DOCS], F32, name="best%d" % t) for t in range(2, TILES)}
+        pair = {t: keep.tile([P, 2, 2 * DOCS], F32, name="pair%d" % t) for t in (0, 2, 3)}
         y_all = keep.tile([P, TILES, 2 * DOCS], F32, name="y_all", align_bytes=ALIGN)
         y = [y_all[:, t, :] for t in range(TILES)]
         both, halves = slice(0, 2 * DOCS), [slice(0, DOCS), slice(DOCS, 2 * DOCS)]
         late = placed.tile([P, 7, 2, DOCS], F32, name="late", offset=LOW_AT, align_bytes=ALIGN)
-        paired = [(0, 1), (1, 1)] + [(t, h) for t in range(2, TILES) for h in range(2)]
+        paired = [(0, 1)] + [(t, h) for t in range(2, TILES) for h in range(2)]
         low = {bank: late[:, i, :, :] for i, bank in enumerate(paired)}
-        best[0] = late[:, 6, :, :].rearrange("p h v -> p (h v)")
+        for t in range(2):
+            best[t] = late[:, len(paired) + t, :, :].rearrange("p h v -> p (h v)")
         whole = {}
 
-        def reduce_whole(t):
-            whole[t] = placed.tile([P, DOCS], F32, name="whole%d" % t, offset=LAST_AT - 4 * DOCS * (1 - t), align_bytes=ALIGN)
-            nc.vector.tensor_reduce(whole[t][:], acc[t, 0][:].rearrange("p (v d) -> p v d", d=D), mybir.AxisListType.X, ALU.max)
+        def reduce_whole(t, h):
+            nc.vector.tensor_reduce(whole[t, h][:], acc[t, h][:].rearrange("p (v d) -> p v d", d=D), mybir.AxisListType.X, ALU.max)
 
         def pairs(t, h):
             tokens = acc[t, h][:].rearrange("p (v d) -> p d v", d=D)
@@ -172,19 +172,22 @@ def tile_picked_ysplade_max_p_kernel(tc, x_words, x_scales, w1, bias, offs, out)
             log_of(t, docs)
             nc.sync.dma_start(out[P * t : P * (t + 1), docs], y[t][:, docs])
 
-        reduce_whole(0)
+        whole[0, 0] = placed.tile([P, DOCS], F32, name="whole00", offset=LAST_AT - 4 * DOCS, align_bytes=ALIGN)
+        reduce_whole(0, 0)
         quantise([2])
-        reduce_whole(1)
+        whole[1, 0] = placed.tile([P, DOCS], F32, name="whole10", offset=LAST_AT, align_bytes=ALIGN)
+        reduce_whole(1, 0)
         quantise([3])
+        whole[1, 1] = placed.tile([P, DOCS], F32, name="whole11", offset=LAST_AT + 4 * PACK * P, align_bytes=ALIGN)
+        reduce_whole(1, 1)
         products(2, range(4))
         products(3, range(4))
-        nc.scalar.activation(best[0][:, halves[0]], whole[0][:], ACT.Relu, bias=b_col[:, 0:1])
         pairs(0, 1)
-        nc.vector.tensor_scalar(best[1][:, halves[0]], whole[1][:], b_col[:, 1:2], 0.0, ALU.add, ALU.max)
-        pairs(1, 1)
-        largest(0, halves[1])
+        for t in range(2):
+            nc.scalar.activation(best[t][:, halves[0]], whole[t, 0][:], ACT.Relu, bias=b_col[:, t : t + 1])
+        nc.vector.tensor_scalar(best[1][:, halves[1]], whole[1, 1][:], b_col[:, 1:2], 0.0, ALU.add, ALU.max)
         pairs(2, 0)
-        largest(1, halves[1])
+        largest(0, halves[1])
         pairs(2, 1)
         largest(2, halves[0])
         pairs(3, 0)

@@ -126,8 +126,13 @@ def tile_picked_ysplade_max_p_kernel(tc, x_words, x_scales, w1, bias, offs, out)
 
         x_first = keep.tile([P, HALF], U32, name="x_first", align_bytes=ALIGN)
         gather(x_first, 0, HALF)
-        round_weights(w_first[:], 0)
-        quantise([0])
+        w_codes[0] = keep.tile([P, P], U32, name="w_codes0", align_bytes=ALIGN)[:]
+        w_sc[0] = keep.tile([P, P], U8, name="w_sc0", align_bytes=ALIGN)[:]
+        for part in (slice(0, P // 2), slice(P // 2, P)):
+            round_weights(w_first[:, :, part], part.start)
+            nc.vector.quantize_mx(
+                out=w_codes[0][:, part].bitcast(FP8X4), scales=w_sc[0][:, part], in_=rounded[:, part, :].rearrange("p m j -> p (m j)")
+            )
         x_third = placed.tile([P, QUARTER], U32, name="x_third", offset=FIRST_AT, align_bytes=ALIGN)
         gather(x_third, HALF, QUARTER)
         round_weights(w_middle[:, :, :P], P)
@@ -185,13 +190,13 @@ def tile_picked_ysplade_max_p_kernel(tc, x_words, x_scales, w1, bias, offs, out)
         pairs(0, 1)
         for t in range(2):
             nc.scalar.activation(best[t][:, halves[0]], whole[t, 0][:], ACT.Relu, bias=b_col[:, t : t + 1])
-        nc.vector.tensor_scalar(best[1][:, halves[1]], whole[1, 1][:], b_col[:, 1:2], 0.0, ALU.add, ALU.max)
         pairs(2, 0)
         largest(0, halves[1])
         pairs(2, 1)
         largest(2, halves[0])
         pairs(3, 0)
         pairs(3, 1)
+        nc.scalar.activation(best[1][:, halves[1]], whole[1, 1][:], ACT.Relu, bias=b_col[:, 1:2])
         log_of(0, both)
         log_of(1, both)
         nc.sync.dma_start(out[: 2 * P, :].rearrange("(t p) v -> p t v", p=P), y_all[:, :2, :])

from contextlib import ExitStack

import concourse.mybir as mybir
from concourse.masks import make_identity

K, T, S, N, D = 512, 4096, 1024, 512, 4
FLOPS = 2 * K * N * S

F32 = mybir.dt.float32
BF16 = mybir.dt.bfloat16
I32 = mybir.dt.int32
U32 = mybir.dt.uint32
U16 = mybir.dt.uint16
U8 = mybir.dt.uint8
FP8X4 = mybir.dt.float8_e4m3fn_x4
ACT = mybir.ActivationFunctionType
ALU = mybir.AluOpType

P = 128
PACK = 4
HALF = 512
QUARTER = HALF // 2
DOCS = HALF // D
TILES = N // P
LIST_GROUP = 16
QUADRANT = 32
SCALE_ROWS = 4
TABLE_ROW = P - K // 32
RUN = 4
ALIGN = 256
MIDDLE = P
LAST = N - P - MIDDLE

FIRST_AT = 0
MIDDLE_AT = FIRST_AT + 4 * PACK * P
LAST_AT = MIDDLE_AT + 4 * PACK * MIDDLE
TABLE_AT = LAST_AT
LOW_AT = LAST_AT + 4 * PACK * LAST - ALIGN


def tile_picked_ysplade_max_p_kernel(tc, x_words, x_scales, w1, bias, offs, out):
    nc = tc.nc
    with ExitStack() as ctx:
        keep = ctx.enter_context(tc.tile_pool(name="keep", bufs=1))
        placed = ctx.enter_context(tc.tile_pool(name="placed", bufs=1))
        psum = ctx.enter_context(tc.psum_pool(name="psum", bufs=1))

        scale_table = placed.tile([P, T], U8, name="scale_table", offset=TABLE_AT, align_bytes=ALIGN)
        nc.sync.dma_start(scale_table[TABLE_ROW:, :].bitcast(I32), x_scales[0].bitcast(I32))
        nc.vector.memset(scale_table[:TABLE_ROW, :].bitcast(I32), 0)
        offsets = keep.tile([P, S // LIST_GROUP], U16, name="offsets")
        nc.sync.dma_start(offsets[:], offs)
        b_rows = keep.tile([P, P], F32, name="b_rows")
        nc.scalar.dma_start(b_rows[P - TILES :, :], bias.rearrange("(t p) o -> t (p o)", p=P))
        word_table = keep.tile([P, T], I32, name="word_table", align_bytes=ALIGN)
        nc.sync.dma_start(word_table[:], x_words[0].rearrange("p n t -> p (n t)").bitcast(I32))
        w_rows = w1.rearrange("(p j) n -> p j n", j=PACK)
        w_first = placed.tile([P, PACK, P], F32, name="w_first", offset=FIRST_AT, align_bytes=ALIGN)
        nc.sync.dma_start(w_first[:], w_rows[:, :, :P])
        w_middle = placed.tile([P, PACK, MIDDLE], F32, name="w_middle", offset=MIDDLE_AT, align_bytes=ALIGN)
        nc.sync.dma_start(w_middle[:], w_rows[:, :, P : P + MIDDLE])

        nc.vector.memset(b_rows[: P - TILES, :], 0.0)
        identity = keep.tile([P, P], F32, name="identity")
        nc.vector.memset(identity[:], 0.0)
        make_identity(nc, identity[:], nomemset=True)
        b_turned = psum.tile([P, P], F32, name="b_turned", tag="acc%d_%d" % (TILES - 1, 1))
        nc.tensor.transpose(b_turned[:], b_rows[:], identity[:])
        b_col = keep.tile([P, TILES], F32, name="b_col")
        nc.scalar.copy(b_col[:], b_turned[:, P - TILES :])

        one = keep.tile([P, 1], F32, name="one")
        nc.vector.memset(one[:], 1.0)
        warm = keep.tile([P, 1], F32, name="warm")
        nc.scalar.activation(warm[:], one[:], ACT.Ln)

        picked_sc = keep.tile([P, S], U8, name="picked_sc", align_bytes=ALIGN)
        nc.vector.tensor_copy(picked_sc[:], scale_table[:].indirect(offsets[:]))
        x_sc = keep.tile([P, S], U8, name="x_sc", align_bytes=ALIGN)
        nc.vector.memset(x_sc[:].bitcast(I32), 0)
        for quad in range(P // QUADRANT):
            source = TABLE_ROW + SCALE_ROWS * quad
            (nc.sync, nc.scalar)[quad % 2].dma_start(
                x_sc[QUADRANT * quad : QUADRANT * quad + SCALE_ROWS, :].bitcast(I32),
                picked_sc[source : source + SCALE_ROWS, :].bitcast(I32),
            )
        w_last = {}
        for t in (2, 3):
            w_last[t] = placed.tile([P, PACK, P], F32, name="w_last%d" % t, offset=LAST_AT + 4 * PACK * P * (t - 2), align_bytes=ALIGN)
            nc.sync.dma_start(w_last[t][:], w_rows[:, :, P * t : P * (t + 1)])

        x_codes, w_codes, w_sc, acc = {}, {}, {}, {}
        rounded = keep.tile([P, N, PACK], BF16, name="rounded", align_bytes=ALIGN)

        def gather(into, first, entries):
            columns = slice(first // LIST_GROUP, (first + entries) // LIST_GROUP)
            nc.vector.tensor_copy(into[:], word_table[:].bitcast(U32).indirect(offsets[:, columns]))
            for q in range(entries // QUARTER):
                x_codes[first // QUARTER + q] = into[:, QUARTER * q : QUARTER * (q + 1)]

        def round_weights(raw, first):
            into = rounded[:, first : first + raw.shape[2], :]
            nc.scalar.copy(into.rearrange("p (c i) j -> p c j i", i=RUN), raw.rearrange("p j (c i) -> p c j i", i=RUN))

        def quantise(tiles):
            codes = keep.tile([P, P * len(tiles)], U32, name="w_codes%d" % tiles[0], align_bytes=ALIGN)
            scales = keep.tile([P, P * len(tiles)], U8, name="w_sc%d" % tiles[0], align_bytes=ALIGN)
            columns = rounded[:, P * tiles[0] : P * (tiles[-1] + 1), :]
            nc.vector.quantize_mx(out=codes[:].bitcast(FP8X4), scales=scales[:], in_=columns.rearrange("p m j -> p (m j)"))
            for i, t in enumerate(tiles):
                w_codes[t], w_sc[t] = codes[:, P * i : P * (i + 1)], scales[:, P * i : P * (i + 1)]

        def products(t, quarters):
            for q in quarters:
                if q % 2 == 0:
                    acc[t, q // 2] = psum.tile([P, HALF], F32, name="acc%d_%d" % (t, q // 2), tag="acc%d_%d" % (t, q // 2))
                nc.tensor.matmul_mx(
                    out=acc[t, q // 2][:, QUARTER * (q % 2) : QUARTER * (q % 2 + 1)],
                    lhsT=w_codes[t].bitcast(FP8X4),
                    lhsT_scale=w_sc[t],
                    rhs=x_codes[q].bitcast(FP8X4),
                    rhs_scale=x_sc[:, QUARTER * q : QUARTER * (q + 1)],
                    start=True,
                    stop=True,
                )

        x_first = keep.tile([P, HALF], U32, name="x_first", align_bytes=ALIGN)
        gather(x_first, 0, HALF)
        w_codes[0] = keep.tile([P, P], U32, name="w_codes0", align_bytes=ALIGN)[:]
        w_sc[0] = keep.tile([P, P], U8, name="w_sc0", align_bytes=ALIGN)[:]
        for part in (slice(0, P // 2), slice(P // 2, P)):
            round_weights(w_first[:, :, part], part.start)
            nc.vector.quantize_mx(
                out=w_codes[0][:, part].bitcast(FP8X4), scales=w_sc[0][:, part], in_=rounded[:, part, :].rearrange("p m j -> p (m j)")
            )
        x_third = placed.tile([P, QUARTER], U32, name="x_third", offset=FIRST_AT, align_bytes=ALIGN)
        gather(x_third, HALF, QUARTER)
        round_weights(w_middle[:, :, :P], P)
        quantise([1])
        x_fourth = placed.tile([P, QUARTER], U32, name="x_fourth", offset=MIDDLE_AT, align_bytes=ALIGN)
        gather(x_fourth, HALF + QUARTER, QUARTER)
        round_weights(w_last[2][:], 2 * P)
        round_weights(w_last[3][:], 3 * P)
        products(0, range(3))
        products(1, range(2))
        products(0, [3])
        products(1, [2, 3])

        best = {t: keep.tile([P, 2 * DOCS], F32, name="best%d" % t) for t in range(2, TILES)}
        pair = {t: keep.tile([P, 2, 2 * DOCS], F32, name="pair%d" % t) for t in (0, 2, 3)}
        y_all = keep.tile([P, TILES, 2 * DOCS], F32, name="y_all", align_bytes=ALIGN)
        y = [y_all[:, t, :] for t in range(TILES)]
        both, halves = slice(0, 2 * DOCS), [slice(0, DOCS), slice(DOCS, 2 * DOCS)]
        late = placed.tile([P, 7, 2, DOCS], F32, name="late", offset=LOW_AT, align_bytes=ALIGN)
        paired = [(0, 1)] + [(t, h) for t in range(2, TILES) for h in range(2)]
        low = {bank: late[:, i, :, :] for i, bank in enumerate(paired)}
        for t in range(2):
            best[t] = late[:, len(paired) + t, :, :].rearrange("p h v -> p (h v)")
        whole = {}

        def reduce_whole(t, h):
            nc.vector.tensor_reduce(whole[t, h][:], acc[t, h][:].rearrange("p (v d) -> p v d", d=D), mybir.AxisListType.X, ALU.max)

        def pairs(t, h):
            tokens = acc[t, h][:].rearrange("p (v d) -> p d v", d=D)
            b = b_col[:, t : t + 1]
            nc.scalar.activation(low[t, h], tokens[:, 0:2, :], ACT.Relu, bias=b)
            nc.vector.scalar_tensor_tensor(pair[t][:, :, halves[h]], tokens[:, 2:4, :], b, low[t, h], ALU.add, ALU.max)

        def largest(t, docs):
            nc.vector.tensor_tensor(best[t][:, docs], pair[t][:, 0, docs], pair[t][:, 1, docs], ALU.max)

        def log_of(t, docs):
            nc.scalar.activation(y[t][:, docs], best[t][:, docs], ACT.Ln, bias=1.0)

        def finish(t, docs):
            log_of(t, docs)
            nc.sync.dma_start(out[P * t : P * (t + 1), docs], y[t][:, docs])

        whole[0, 0] = placed.tile([P, DOCS], F32, name="whole00", offset=LAST_AT - 4 * DOCS, align_bytes=ALIGN)
        reduce_whole(0, 0)
        quantise([2])
        whole[1, 0] = placed.tile([P, DOCS], F32, name="whole10", offset=LAST_AT, align_bytes=ALIGN)
        reduce_whole(1, 0)
        quantise([3])
        whole[1, 1] = placed.tile([P, DOCS], F32, name="whole11", offset=LAST_AT + 4 * PACK * P, align_bytes=ALIGN)
        reduce_whole(1, 1)
        products(2, range(4))
        products(3, range(4))
        pairs(0, 1)
        for t in range(2):
            nc.scalar.activation(best[t][:, halves[0]], whole[t, 0][:], ACT.Relu, bias=b_col[:, t : t + 1])
        pairs(2, 0)
        largest(0, halves[1])
        pairs(2, 1)
        largest(2, halves[0])
        pairs(3, 0)
        pairs(3, 1)
        nc.scalar.activation(best[1][:, halves[1]], whole[1, 1][:], ACT.Relu, bias=b_col[:, 1:2])
        log_of(0, both)
        log_of(1, both)
        nc.sync.dma_start(out[: 2 * P, :].rearrange("(t p) v -> p t v", p=P), y_all[:, :2, :])
        log_of(2, halves[0])
        largest(2, halves[1])
        log_of(2, halves[1])
        nc.sync.dma_start(out[2 * P : 3 * P, :], y[2])
        for h in range(2):
            largest(3, halves[h])
            finish(3, halves[h])
